import numpy as np, ml_dtypes
CORES = [1,5,17,21,33,37,49,53]
N = 8
BF = ml_dtypes.bfloat16
V, L, M, S, RO, E = 4096, 128, 32, 6, 2, 20
def pack(X, w, Q, T):
    return {"ent": np.ascontiguousarray(np.transpose(X, (0, 1, 3, 2)).reshape(N, 128, V)).astype(np.float32).astype(BF), "hw": np.reshape(w, (N, 128, 1)).astype(np.int32),
            "mix": np.reshape(Q, (N, 128, 16)).astype(np.float32).astype(BF), "goal": np.reshape(T, (N, 128, 1)).astype(np.int32)}
def genes(rng, p):
    return np.where(rng.random((N, 8, V, 16)) < p, rng.integers(1, 256, (N, 8, V, 16)), 0)
def aims(rng, Q):
    return np.matmul(rng.integers(1, 256, (N, 8, 1, 16)), Q)[:, :, 0]
def parts(rng):
    share = rng.choice(np.array([0.2, 0.3, 0.4, 0.55]), (N, 8, 1, 1))
    X = genes(rng, share * (0.5 + rng.random((N, 8, V, 1)))); w = rng.integers(1, 256, (N, 8, 16)); Q = rng.integers(-8, 9, (N, 8, 16, 16))
    return X, w, Q, aims(rng, Q)
def spot(x, w):
    u = np.matmul(x, w) & 4095
    return V // 2 + (((u * u >> 5) + 37 * u) & (V // 2 - 1))
def setup_inputs(rng):
    return pack(*parts(rng))
def setup_inputs_ends(rng):
    share = rng.choice(np.array([0.1, 0.2, 0.4, 0.7]), (N, 8, 1, 1)); share[:, 5] = 0.08; share[:, 6:] = 0.6
    X = 255 * (rng.random((N, 8, V, 16)) < share * (0.5 + rng.random((N, 8, V, 1)))).astype(np.int64)
    w = np.where(rng.random((N, 8, 16)) < 0.5, 1, 255)
    for g in (3, 6): w[:, g] = 255
    for g in (1, 7): w[:, g, :2] = 1; w[:, g, 2] = 255
    Q = 16 * rng.integers(0, 2, (N, 8, 16, 16)) - 8; Q[:, 5:] = 8
    T = 65280 * rng.integers(0, 2, (N, 8, 16)) - 32640; T[:, 5] = -32640
    T[1::2, 7] = -32640; T[0::2, 7] = 32640; T[1::2, 6] = 32640; T[0::2, 6] = -32640
    X[:, :, V - 1] = 255; X[:, :, V - 2] = 0
    for t in range(RO):
        for i in (0, 3, L - 1):
            for g in (1, 7): X[:, g, L * t + i] = 0; X[:, g, L * t + i, :3] = 255
            X[:, 6, L * t + i] = 255
        for i in (2, L - 2): X[:, 7, L * t + i] = 255; X[:, 6, L * t + i] = 0
    return pack(X, w, Q, T)
def setup_inputs_spread(rng):
    p = 1.3 * np.sqrt(rng.random((N, 8, V, 1))) * rng.random((N, 8, 1, 16))
    X = np.where(rng.random((N, 8, V, 16)) < p, np.minimum(np.exp2(8 * rng.random((N, 8, V, 16))).astype(np.int64), 255), 0)
    w = np.minimum(np.exp2(8 * rng.random((N, 8, 16))).astype(np.int64), 255)
    Q = rng.integers(-8, 9, (N, 8, 16, 16)) * (rng.random((N, 8, 16, 16)) < 0.2 + rng.random((N, 8, 16, 1)))
    T = np.clip(((2 * rng.random((N, 8, 16)) - 1) * np.exp2(10 + 5 * rng.random((N, 8, 16)))).astype(np.int64), -32640, 32640)
    return pack(X, w, Q, T)
def setup_inputs_corners(rng):
    X, w, Q, T = parts(rng); H = V // 2; full = rng.integers(1, 256, (N, 8, V, 16)); one = np.arange(16)[None, :] == rng.integers(0, 16, (H, 1))
    for r in range(N):
        for g in range(8):
            k = (g + r) % 8
            if k == 0: X[r, g] = full[r, g]
            if k == 1: X[r, g] = np.where(rng.random((V, 16)) < 0.02, full[r, g], 0)
            if k == 2: w[r, g] = 1
            if k == 3: w[r, g] = 255
            if k == 4: X[r, g, :H] = full[r, g, :H]; X[r, g, H:] = 0
            if k == 5: X[r, g, :H] = np.where(one, full[r, g, :H], 0); X[r, g, H:] = full[r, g, H:]
            if k == 6: Q[r, g] = 0; T[r, g] = 0
            if k == 7: X[r, g, :H, :8] = full[r, g, :H, :8]; X[r, g, :H, 8:] = 0; X[r, g, H:, :8] = 0; X[r, g, H:, 8:] = full[r, g, H:, 8:]
    return pack(X, w, Q, T)
def setup_inputs_alike(rng):
    X, w, Q, T = parts(rng); n = rng.choice(np.array([4, 12, 40]), (N, 8, 1)); n[:, 0] = 4; n[:, 1] = 40
    pick = (n * rng.random((N, 8, V))).astype(np.int64)
    return pack(np.take_along_axis(X[:, :, :40], np.minimum(pick, n - 1)[..., None], 2), w, Q, T)
def setup_inputs_close(rng):
    X, w, Q, T = parts(rng); H = V // 2; K = RO * L
    F = int(rng.integers(0, N)); Z = (F + 1) % N
    X[F] = rng.integers(1, 256, (8, V, 16))
    sub = np.zeros((16384, 16), np.int64); sub[:, 0] = 255; sub[:, 1:15] = 255 * ((np.arange(16384)[:, None] >> np.arange(14)[None, :]) & 1)
    for r in range(N):
        for g in range(8):
            s = int(rng.choice(np.array([-1, 1])))
            if g in (0, 7):
                Q[r, g, 0] = 0; Q[r, g, 0, 0] = -s; Q[r, g, 1:5] = -8 * s; Q[r, g, 5:] = s * rng.integers(0, 3, (11, 16)); T[r, g] = 32640 * s
            elif g in (1, 2):
                Q[r, g] = 8 * s; Q[r, g, 0, 1:] = 0; T[r, g] = 32640 * s; T[r, g, 0] = -32640 * s
            elif g == 3:
                z = rng.choice(np.array([-1, 1]), 16); Q[r, g] = 8 * z; T[r, g] = -32640 * z
            else:
                Q[r, g] = 8; T[r, g] = 32640
            if r == F: continue
            if g == 3:
                X[r, g, :K] = 255; X[r, g, :K, :15] -= rng.integers(0, 2, (K, 15))
                X[r, g, H:] = 254; X[r, g, H:, :15] -= rng.integers(0, 2, (H, 15))
                continue
            c = sub[15::16] if g in (0, 7) else sub
            X[r, g, H:] = 255; X[r, g, H:, 0] = 254 if g in (0, 7) else rng.integers(240 if g < 3 else 192, 255, H)
            if r == Z and g in (4, 5, 6):
                c = np.array(c); c[:, 0] = 254; X[r, g, H:, 0] = 255
            b = spot(c, w[r, g]); o = rng.permutation(np.unique(b, return_index=True)[1])
            e = np.concatenate([o, rng.choice(o[1:], L)])[:L]
            if g in (0, 7): e[0] = np.argmax(b)
            if g == 4: e[:] = e[0]
            if g == 6: e[L - 1] = e[0]
            X[r, g, :K] = c[rng.choice(o, K)]; X[r, g, :L] = c[e]
    return pack(X, w, Q, T)
def check_inputs(d):
    bad = []
    for k, lo, hi in (("ent", 0, 255), ("hw", 1, 255), ("mix", -8, 8), ("goal", -32640, 32640)):
        v = np.asarray(d[k]).astype(np.float64)
        if not np.all((v >= lo) & (v <= hi)): bad.append("range of " + k)
        elif np.any(v != np.floor(v)): bad.append("whole numbers of " + k)
    return bad
def reference(ent, hw, mix, goal):
    X = np.ascontiguousarray(np.transpose(np.asarray(ent).astype(np.float32).reshape(N, 8, 16, V), (0, 1, 3, 2)))
    w = hw.astype(np.float32).reshape(N, 8, 16, 1); Q = mix.astype(np.float32).reshape(N, 8, 16, 16); T = goal.astype(np.float32).reshape(N, 8, 1, 16)
    gr = np.arange(8)[:, None]; m = np.tile(np.arange(M), L); low = np.tri(L, L, -1, dtype=bool)
    def hash12(s, z): return np.matmul(z, w[s])[..., 0].astype(np.int64) & 4095
    def misfit(s, z): return np.add.reduce(np.abs(np.matmul(z, Q[s]) - T[s]), axis=-1)
    for t in range(RO):
        new = np.array(X)
        for r in range(N):
            q = (r + 1 + t % (N - 1)) % N
            A = X[r, :, L * t:L * t + L]; u = hash12(r, A)
            b = V // 2 + (((u * u >> 5) + 37 * u) & (V // 2 - 1)); B = X[r][gr, b]; AB = np.where(A == 0, B, A)
            first = np.logical_not(np.any((b[:, :, None] == b[:, None, :]) & low, axis=2))
            A2 = np.repeat(A, M, axis=1); B2 = np.repeat(B, M, axis=1); AB2 = np.repeat(AB, M, axis=1); c = np.zeros_like(A2)
            for d in range(S):
                v = hash12(q, np.where(c == 0, A2, c))
                h = ((v * v >> 5) + (2 * m + 1) * v + 811 * d) & (V - 1)
                p = X[q][gr, h]; c = np.where(c == 0, p, c)
            fa, fb, fab = [misfit(q, np.where(e == 0, c, e)) for e in (A2, B2, AB2)]
            count = np.add.reduce((fab > np.minimum(fa, fb)).reshape(8, L, M).astype(np.int64), axis=2)
            donor = p.reshape(8, L, M, 16)[:, :, 0]
            ga, la = np.nonzero((count <= E + (u & 1)) & first); ba = b[ga, la]
            new[r, ga, L * t + la] = AB[ga, la]; new[r, ga, ba] = donor[ga, la]
        X = new
    return {"y": np.ascontiguousarray(np.transpose(X, (0, 1, 3, 2))).reshape(N, 128, V).astype(BF)}

@@ -1,0 +1,568 @@
+from concourse.bass import DstId, RemoteDMATransfer
+from concourse.mybir import dt, AluOpType, AxisListType, ActivationFunctionType
+
+ALU = AluOpType
+ACT = ActivationFunctionType
+N, V, L, RO, S = 8, 4096, 128, 2, 6
+H = V // 2
+CH = [(0, 8), (8, 8), (16, 16)]
+BIAS = [13000.0, 4000.0, 2000.0, 0.0]
+G0ENG = ["dve", "act"] * 4
+GS = 512
+CDMA = True
+DELTA = 12.5 / 32
+CY, PCY, HOP, GA, WINDOW = 1.04, 0.52, 110.0, 1.56, 30.0
+NC = 4
+VB = 0.0
+
+BF, F32, I32, U16 = "bfloat16", "float32", "int32", "uint16"
+SCRATCH = {
+    "ps": ("psum", [128, 4096], F32),
+    "tab": ("sbuf", [128, V + L], BF),
+    "hwi": ("sbuf", [128, 4], I32), "goi": ("sbuf", [128, 4], I32), "mixs": ("sbuf", [128, 16], BF),
+    "wf": ("sbuf", [128, 1], F32), "negt": ("sbuf", [128, 1], F32),
+    "ones": ("sbuf", [128, 1024], BF), "onef": ("sbuf", [128, 128], F32),
+    "ident": ("sbuf", [128, 128], BF), "identf": ("sbuf", [128, 128], F32),
+    "i256": ("sbuf", [128, 128], BF), "ineg": ("sbuf", [128, 128], BF),
+    "b16a": ("sbuf", [128, 128], BF), "b16": ("sbuf", [128, 128], BF), "bmf": ("sbuf", [128, 8], F32),
+    "wblk": ("sbuf", [128, 128], BF), "w8": ("sbuf", [128, 16], BF), "qblk": ("sbuf", [128, 128], BF),
+    "sel": ("sbuf", [128, 128], F32), "ob": ("sbuf", [128, 40], F32),
+    "sg": ("sbuf", [128, 1024], BF), "big": ("sbuf", [128, 128], BF), "upp": ("sbuf", [128, 128], BF),
+    "z2": ("sbuf", [128, 240], BF),
+    "pi": ("sbuf", [128, 4], I32), "mo": ("sbuf", [128, NC], F32),
+    "acol": ("sbuf", [128, NC], F32), "k0": ("sbuf", [128, NC], F32), "kcol": ("sbuf", [128, 6 * NC], F32),
+    "mi": ("sbuf", [128, 256], I32), "m16": ("sbuf", [128, 256], F32), "rst": ("sbuf", [128, 256], F32),
+    "dump": ("sbuf", [128, 256], F32),
+    "ui": ("sbuf", [128, 256], I32), "upar": ("sbuf", [128, 256], I32), "thr": ("sbuf", [128, 256], BF),
+    "uf": ("sbuf", [128, 256], F32), "bi": ("sbuf", [128, 256], I32), "bfl": ("sbuf", [128, 256], F32),
+    "xy": ("sbuf", [128, 512], BF), "nxy": ("sbuf", [128, 512], BF), "t1": ("sbuf", [128, 256], F32),
+    "t2": ("sbuf", [128, 256], F32), "t3": ("sbuf", [128, 256], F32), "t4": ("sbuf", [128, 256], F32),
+    "offb": ("sbuf", [128, 16], U16), "offs": ("sbuf", [128, 16], U16),
+    "eq": ("sbuf", [128, 2048], BF), "fst": ("sbuf", [128, 256], BF),
+    "ma": ("sbuf", [128, 256], BF), "daf": ("sbuf", [128, 256], BF), "d1": ("sbuf", [128, 128], BF),
+    "pk0": ("sbuf", [128, 256], BF), "pk1": ("sbuf", [128, 256], BF),
+    "lb0": ("sbuf", [128, 256], BF), "lb1": ("sbuf", [128, 256], BF),
+    "la0": ("sbuf", [128, 128], BF), "la1": ("sbuf", [128, 128], BF),
+    "ret0": ("sbuf", [128, 256], BF), "ret1": ("sbuf", [128, 256], BF),
+    "lr0": ("sbuf", [128, 256], BF), "lr1": ("sbuf", [128, 256], BF),
+    "arep0": ("sbuf", [128, 2048], BF), "arep1": ("sbuf", [128, 2048], BF),
+    "ah0": ("sbuf", [128, 128], BF), "ah1": ("sbuf", [128, 128], BF), "aht": ("sbuf", [128, 128], BF),
+    "rep": ("sbuf", [128, 1024], BF), "msk": ("sbuf", [128, 1536], BF),
+    "nb": ("sbuf", [128, S * V], BF), "yb": ("sbuf", [128, V], BF), "xs": ("sbuf", [128, 3 * V], BF),
+    "ab": ("sbuf", [128, 9 * 512], F32),
+    "cs": ("sbuf", [128, 128 * NC], F32), "xi": ("sbuf", [128, 256 * NC], I32), "vf": ("sbuf", [128, 256 * NC], F32),
+    "v8": ("sbuf", [128, 64], I32), "v16": ("sbuf", [128, 128], I32), "hf": ("sbuf", [128, 256 * NC], F32),
+    "pad": ("sbuf", [128, 2 * NC * 17, 8], F32), "off": ("sbuf", [128, 256], U16),
+    "o00": ("sbuf", [128, 256], U16), "o01": ("sbuf", [128, 256], U16),
+    "wg": ("sbuf", [128, 128], BF), "worse": ("sbuf", [128, 16, 16], BF), "wt": ("sbuf", [128, 256], BF),
+    "don": ("sbuf", [128, 128], BF), "fz": ("sbuf", [128, 128], BF), "ta": ("sbuf", [128, 128], BF),
+    "tb": ("sbuf", [128, 128], BF),
+}
+DMAS = ["lA", "lhw", "lhi", "llo", "lgo", "lmx", "ylo", "yA0", "yA1", "yhi"]
+ADDS = ["ad%d%d%d" % (t, c, d) for t in range(RO) for c in range(len(CH)) for d in range(1, S - 1)] if CDMA else []
+REMS = ["A0", "A1", "B0", "B1", "R0", "R1"]
+SEMAPHORES = ["cpe", "cdve", "cact", "cpool"] + DMAS + ADDS + ["r" + n for n in REMS] + ["s" + n for n in REMS]
+
+
+def build(g, core, T, topo, assign):
+    rank = T.rank_of(core)
+    ops = []
+    ve, sc, pe = g.vector, g.scalar, g.tensor
+    ps = T.ps
+    bias, nl = [0.0], [0]
+
+    def add(eng, fns, dur, r, w, banks=(), kind="c", sem=None, cnt=0, land=(), lat=0.0):
+        ops.append(dict(eng=eng, fns=fns, dur=dur, r=list(r), w=list(w), banks=list(banks), kind=kind,
+                        sem=sem, cnt=cnt, land=list(land), lat=lat, bias=bias[0]))
+
+    def lease():
+        nl[0] += 1
+        k = "L%d" % nl[0]
+        return k, 512 * assign.get(k, 0)
+
+    def vd(n, c=1.0):
+        return 40 + max(64, n * c) * CY
+
+    def ts(out, in0, s1, op0, r, w, n, s2=None, op1=None, banks=(), c=1.0):
+        if op1 is None:
+            add("dve", [lambda: ve.tensor_scalar(out, in0, s1, None, op0)], vd(n, c), r, w, banks)
+        else:
+            add("dve", [lambda: ve.tensor_scalar(out, in0, s1, s2, op0, op1)], vd(n, c), r, w, banks)
+
+    def tt(out, a, b, op, r, w, n, banks=(), c=2.0):
+        add("dve", [lambda: ve.tensor_tensor(out, a, b, op)], vd(n, c), r, w, banks)
+
+    def cp(out, a, r, w, n, banks=(), c=1.0):
+        add("dve", [lambda: ve.tensor_copy(out, a)], vd(n, c), r, w, banks)
+
+    def ms(out, val, w, n):
+        add("dve", [lambda: ve.memset(out, val)], vd(n, 0.5), [], w)
+
+    def act(out, a, f, r, w, n, banks=(), c=1.0, **kw):
+        add("act", [lambda: sc.activation(out, a, f, **kw)], 60 + max(64, n * c) * CY, r, w, banks)
+
+    def mm(lst, r, w, banks=()):
+        fns, dur = [], 30.0
+        for (o, l, x, st, sp, cyc) in lst:
+            fns.append(lambda o=o, l=l, x=x, st=st, sp=sp: pe.matmul(o, l, x, st, sp))
+            dur += cyc * PCY
+        add("pe", fns, dur, r, w, banks)
+
+    def dma(q, out, a, r, w, sem, lat):
+        qq = g.sync if q == "sp" else sc
+        add(q, [lambda: qq.dma_start(out, a)], 60, r, w, kind="d", sem=sem, cnt=16, lat=lat)
+
+    def send(name, dst, out, a, r, land, part, lat):
+        es = topo.engines(core, dst)[:8]
+        es = es if part is None else es[part::2]
+        m = 0
+        for e in es:
+            m |= 1 << e
+        rid, pid, _ = topo.addr(dst)
+        add("pool", [lambda: g.remote_dma(out, a, T.sem["r" + name], T.sem["s" + name], pid, rid, m)], 300, r, [],
+            kind="r", sem=name, cnt=len(es), land=land, lat=lat)
+
+    def pool(fn, n, r, w):
+        add("pool", [fn], 170 + 2 * n * CY, r, w)
+
+    TAB = ["tA0", "tA1", "tlo", "thi"]
+    judge = [T.cores[(rank + 1 + t % (N - 1)) % N] for t in range(RO)]
+    home = [T.cores[(rank - 1 - t % (N - 1)) % N] for t in range(RO)]
+    la, lb, lr = [T.la0, T.la1], [T.lb0, T.lb1], [T.lr0, T.lr1]
+    pk, ret, arep, ah, o0 = [T.pk0, T.pk1], [T.ret0, T.ret1], [T.arep0, T.arep1], [T.ah0, T.ah1], [T.o00, T.o01]
+    sig = [16 if n == 16 else 8 for (_, n) in CH]
+    nch = len(CH)
+    reg, fill = [], [3072, 3584]
+    for c in range(nch):
+        b = c % 2 if fill[c % 2] + 16 * sig[c] <= (3584, 3968)[c % 2] else 1 - c % 2
+        reg.append((6 + b, fill[b]))
+        fill[b] += 16 * sig[c]
+
+    dma("sp", T.tab[:, 0:256], T.ent[:, 0:256], [], ["tA0", "tA1"], "lA", 2300)
+    dma("act", T.hwi[:, 0:1], T.hw[:], [], ["hwi"], "lhw", 2200)
+    dma("sp", T.tab[:, H:V], T.ent[:, H:V], [], ["thi"], "lhi", 5000)
+    dma("act", T.tab[:, 256:H], T.ent[:, 256:H], [], ["tlo"], "llo", 7000)
+    dma("sp", T.goi[:, 0:1], T.goal[:], [], ["goi"], "lgo", 7000)
+    dma("sp", T.mixs[:], T.mix[:], [], ["mixs"], "lmx", 7000)
+    ms(T.ones[:, 0:128], 1.0, ["ones"], 128)
+    ms(T.ones[:, 128:1024], 1.0, ["onesb"], 896)
+    ms(T.onef[:], 1.0, ["onef"], 256)
+    pool(lambda: g.affine_select(T.b16a[:], T.ones[:, 0:128], [[-16, 8], [0, 16]], ALU.is_ge, 0.0, 0, 1), 128, ["ones"], ["b16a"])
+    pool(lambda: g.affine_select(T.b16[:], T.b16a[:], [[16, 8], [0, 16]], ALU.is_ge, 0.0, 15, -1), 128, ["b16a"], ["b16"])
+    pool(lambda: g.iota(T.pi[:, 0:1], [[0, 1]], 0, 1), 1, [], ["pi"])
+    if 8 in sig:
+        pool(lambda: g.affine_select(T.sel[:], T.onef[:], [[-1, 2], [-2, 64]], ALU.is_equal, 0.0, 0, 1), 128, ["onef"], ["sel"])
+        for c in range(nch):
+            if sig[c] == 8:
+                for tmp in (c, NC + c):
+                    ms(T.pad[:, 17 * tmp:17 * tmp + 17, :], 0.0, ["pad%d" % tmp], 272)
+    pool(lambda: g.affine_select(T.identf[:], T.onef[:], [[-1, 128]], ALU.is_equal, 0.0, 0, 1), 128, ["onef"], ["identf"])
+    send("A0", judge[0], la[0][:], T.tab[:, 0:128], ["tA0"], ["la0"], 0, 3500)
+    pool(lambda: g.iota(T.mi[:], [[-1, 256]], 256, 1), 256, [], ["mi"])
+    send("A1", judge[1], la[1][:], T.tab[:, 128:256], ["tA1"], ["la1"], 1, 3500)
+    ms(T.big[:], 8192.0, ["big"], 128)
+    pool(lambda: g.affine_select(T.upp[:], T.big[:], [[-1, 128]], ALU.is_ge, 0.0, 0, 1), 128, ["big"], ["upp"])
+    pool(lambda: g.affine_select(T.sg[:], T.ones[:], [[-16, 8], [0, 128]], ALU.is_equal, 0.0, 0, 1), 1024, ["ones", "onesb"], ["sg"])
+    pool(lambda: g.iota(T.dump[:], [[0, 2], [1, 128]], H, 0, allow_small_or_imprecise_dtypes=True), 256, [], ["dump"])
+    cp(T.wf[:], T.hwi[:, 0:1], ["hwi"], ["wf"], 1)
+    act(T.wblk[:], T.b16[:], ACT.Identity, ["b16", "wf"], ["wblk"], 128, scale=T.wf[:, 0:1])
+    ts(T.w8[:, 0:8], T.b16[:, 0:128:16], T.wf[:, 0:1], ALU.mult, ["b16", "wf"], ["w8a"], 8)
+    act(T.w8[:, 8:16], T.w8[:, 0:8], ACT.Copy, ["w8a"], ["w8b"], 8, scale=1.0 / 256)
+    for c in range(nch):
+        j = 1 if sig[c] == 8 else 2
+        if sig[c] not in sig[:c]:
+            ts(T.pi[:, j:j + 1], T.pi[:, 0:1], 4 if sig[c] == 8 else 3, ALU.arith_shift_right, ["pi"], ["pi%d" % j], 1)
+        ts(T.mo[:, c:c + 1], T.pi[:, j:j + 1], 2.0, ALU.mult, ["pi%d" % j], ["mo%d" % c], 1, 2.0 * CH[c][0] + 1, ALU.add)
+    MO = ["mo%d" % c for c in range(nch)]
+    act(T.acol[:, 0:nch], T.mo[:, 0:nch], ACT.Copy, MO, ["acol"], nch, scale=16.0)
+    act(T.k0[:, 0:nch], T.mo[:, 0:nch], ACT.Square, MO, ["k0"], nch)
+    for d in range(S):
+        act(T.kcol[:, NC * d:NC * d + nch], T.k0[:, 0:nch], ACT.Identity, ["k0"], ["kcol%d" % d], nch, scale=-8.0, bias=811.0 * d - DELTA)
+    act(T.ident[:], T.identf[:], ACT.Copy, ["identf"], ["ident"], 128)
+    act(T.i256[:], T.identf[:], ACT.Copy, ["identf"], ["i256"], 128, scale=256.0)
+    act(T.ineg[:], T.identf[:], ACT.Copy, ["identf"], ["ineg"], 128, scale=-2.0 ** 21)
+    ts(T.mi[:], T.mi[:], 15, ALU.bitwise_and, ["mi"], ["mi"], 256)
+    ts(T.m16[:], T.mi[:], 0.0, ALU.is_equal, ["mi"], ["m16"], 256)
+    ms(T.rst[:], 1.0, ["rst"], 512)
+    ms(T.rst[:, 0:256:16], 0.0, ["rst"], 32)
+    ms(T.z2[:], 0.0, ["z2"], 240)
+    ms(T.z2[:, 112:128], 1.0, ["z2"], 16)
+    act(T.bmf[:], T.b16[:, 0:128:16], ACT.Copy, ["b16"], ["bmf"], 8)
+    for j, s in ((0, 1.0), (1, 1.0), (2, -1.0), (3, 0.0), (4, -1.0)):
+        act(T.ob[:, 8 * j:8 * j + 8], T.bmf[:], ACT.Copy, ["bmf"], ["ob%d" % j], 8, scale=s)
+    for k in range(8):
+        act(T.qblk[:, 16 * k:16 * k + 16], T.mixs[:], ACT.Identity, ["mixs", "bmf"], ["qb%d" % k], 16, scale=T.bmf[:, k:k + 1])
+    OB, QB = ["ob%d" % j for j in range(5)], ["qb%d" % k for k in range(8)]
+    ts(T.negt[:], T.goi[:, 0:1], -1.0, ALU.mult, ["goi"], ["negt"], 1)
+
+    def chain(c, d, src, srck, tmp, col, kt, banks, dst, dstk):
+        m0, n = CH[c]
+        W, J = 8 * sig[c], 8 * n
+        P = 128 * n // sig[c]
+        xi, vf = T.xi[0:P, 128 * tmp:128 * tmp + W], T.vf[0:P, 128 * tmp:128 * tmp + W]
+        kx, kv, kp = "xi%d" % tmp, "vf%d" % tmp, "pad%d" % tmp
+        ts(vf, src, T.acol[0:P, c:c + 1], ALU.add, [srck, "acol"], [kv], W)
+        act(vf, vf, ACT.Square, [kv], [kv], W)
+        ts(xi, vf, 1.0 / 32, ALU.mult, [kv, "kcol%d" % d], [kx], W, T.kcol[0:P, NC * d + c:NC * d + c + 1], ALU.add)
+        ts(xi, xi, V - 1, ALU.bitwise_and, [kx], [kx], W)
+        tr = ps[:, col:col + J]
+        if sig[c] == 8:
+            b = 17 * tmp
+            cp(T.pad[0:P, b + 1:b + 17:2, :], xi, [kx], [kp], W)
+            mm([(tr, T.pad[0:P, b + 1:b + 17, :], T.sel[0:P, 0:J], True, False, 256),
+                (tr, T.pad[0:P, b:b + 16, :], T.sel[0:P, 64:64 + J], False, True, 256)], [kp, "sel"], [kt], banks)
+        else:
+            hf = T.hf[:, 128 * tmp:128 * tmp + 128]
+            cp(hf, xi, [kx], [kp], W)
+            mm([(tr, hf, T.identf[:], True, True, 512)], [kp, "identf"], [kt], banks)
+        cp(dst[:, 8 * m0:8 * m0 + J], tr, [kt], [dstk, kt], J, banks=banks)
+
+    def step0(t):
+        a, r = la[t], arep[t]
+        k = "arep%d" % t
+        cp(r[:, 0:128], a[:], ["la%d" % t], [k + "a"], 128, c=0.5)
+        cp(r[:, 128:256], a[:], ["la%d" % t], [k + "b"], 128, c=0.5)
+        ks, w = [k + "a", k + "b"], 256
+        while w < 128 * max(sig):
+            cp(r[:, w:2 * w], r[:, 0:w], ks, [k + str(w)], w, c=0.5)
+            ks, w = ks + [k + str(w)], 2 * w
+        for sg_ in sorted(set(sig), reverse=True):
+            kl, col = lease()
+            v, kv = (T.v8, "v8") if sg_ == 8 else (T.v16, "v16")
+            mm([(ps[:, col + s:col + 8 * sg_:sg_], r[:, s:128 * sg_:sg_], T.w8[:, 0:8], True, True, 64) for s in range(sg_)], ks + ["w8a"], [kl])
+            cp(v[:], ps[:, col:col + 8 * sg_], [kl], [kv, kl], 8 * sg_)
+            ts(v[:], v[:], V - 1, ALU.bitwise_and, [kv], [kv], 8 * sg_)
+        for c in range(nch):
+            kl, col = lease()
+            v, kv = (T.v8, "v8") if sig[c] == 8 else (T.v16, "v16")
+            chain(c, 0, v[0:128 * CH[c][1] // sig[c], :], kv, NC + c, col, kl, [], o0[t], "o0%d%d" % (t, c))
+        ts(T.aht[:], a[:], 0.0, ALU.is_equal, ["la%d" % t], ["aht"], 128, 4096.0, ALU.mult, c=0.5)
+        tt(ah[t][:], T.aht[:], a[:], ALU.add, ["aht", "la%d" % t], ["ah%d" % t], 128)
+        return ks
+
+    RA = [step0(0)]
+
+    kl, col = lease()
+    mm([(ps[:, col:col + 256], T.wblk[:], T.tab[:, 0:256], True, True, 256)], ["wblk", "tA0", "tA1"], [kl])
+    cp(T.ui[:], ps[:, col:col + 256], [kl], ["ui", kl], 256)
+    ts(T.ui[:], T.ui[:], V - 1, ALU.bitwise_and, ["ui"], ["ui"], 256)
+    ts(T.uf[:], T.ui[:], 592.0, ALU.add, ["ui"], ["uf"], 256)
+    act(T.uf[:], T.uf[:], ACT.Square, ["uf"], ["uf"], 256)
+    ts(T.bi[:], T.uf[:], 1.0 / 32, ALU.mult, ["uf"], ["bi"], 256, -8.0 * 37 * 37 - DELTA, ALU.add)
+    ts(T.bi[:], T.bi[:], H - 1, ALU.bitwise_and, ["bi"], ["bi"], 256)
+    cp(T.bfl[:], T.bi[:], ["bi"], ["bfl"], 256)
+    act(T.xy[:, 0:256], T.bfl[:], ACT.Copy, ["bfl"], ["xh"], 256)
+    tt(T.xy[:, 256:512], T.bfl[:], T.xy[:, 0:256], ALU.subtract, ["bfl", "xh"], ["xl"], 256)
+    act(T.nxy[:], T.xy[:], ACT.Copy, ["xh", "xl"], ["nxy"], 512, scale=-1.0)
+    for t in range(RO):
+        for hf in range(2):
+            e = 2 * t + hf
+            kl, col = lease()
+            lst = []
+            for k in range(4):
+                gq = 4 * hf + k
+                o = ps[:, col + 128 * k:col + 128 * k + 128]
+                s_ = T.sg[:, 128 * gq:128 * gq + 128]
+                c0, c1 = 128 * t, 256 + 128 * t
+                lst += [(o, s_, T.xy[:, c0:c0 + 128], True, False, 128), (o, s_, T.xy[:, c1:c1 + 128], False, False, 128),
+                        (o, T.nxy[:, c0:c0 + 128], s_, False, False, 128), (o, T.nxy[:, c1:c1 + 128], s_, False, False, 128),
+                        (o, T.ident[:], T.upp[:], False, True, 128)]
+            mm(lst, ["sg", "xh", "xl", "nxy", "ident", "upp"], [kl])
+            ts(T.eq[:, 512 * e:512 * e + 512], ps[:, col:col + 512], 0.0, ALU.is_equal, [kl], ["eq%d" % e, kl], 512)
+        kl, col = lease()
+        o = ps[:, col:col + 128]
+        mm([(o, T.z2[:, 112 - 16 * k:240 - 16 * k], T.eq[:, 1024 * t + 128 * k:1024 * t + 128 * k + 128], k == 0, k == 7, 128) for k in range(8)],
+           ["z2", "eq%d" % (2 * t), "eq%d" % (2 * t + 1)], [kl])
+        ts(T.fst[:, 128 * t:128 * t + 128], o, 0.0, ALU.is_equal, [kl], ["fst%d" % t, kl], 128)
+    tt(T.t1[:], T.bfl[:], T.m16[:], ALU.mult, ["bfl", "m16"], ["t1"], 256)
+    add("dve", [lambda: ve.tensor_tensor_scan(T.t2[:], T.rst[:], T.t1[:], 0.0, ALU.mult, ALU.add)], vd(256), ["t1", "rst"], ["t2"])
+    cp(T.offb[:], T.t2[:, 15:256:16], ["t2"], ["offb"], 16)
+    ts(T.upar[:], T.ui[:], 1, ALU.bitwise_and, ["ui"], ["upar"], 256)
+    ts(T.thr[:], T.upar[:], 20.5, ALU.add, ["upar"], ["thr"], 256)
+    tt(T.t3[:], T.bfl[:], T.dump[:], ALU.subtract, ["bfl", "dump"], ["t3"], 256)
+    tt(T.t3[:], T.t3[:], T.fst[:], ALU.mult, ["t3", "fst0", "fst1"], ["t3"], 256)
+    tt(T.t3[:], T.t3[:], T.dump[:], ALU.add, ["t3", "dump"], ["t3"], 256)
+    tt(T.t3[:], T.t3[:], T.m16[:], ALU.mult, ["t3", "m16"], ["t3"], 256)
+    add("dve", [lambda: ve.tensor_tensor_scan(T.t4[:], T.rst[:], T.t3[:], 0.0, ALU.mult, ALU.add)], vd(256), ["t3", "rst"], ["t4"])
+    cp(T.offs[:], T.t4[:, 15:256:16], ["t4"], ["offs"], 16)
+    ts(T.ma[:], T.tab[:, 0:256], 0.0, ALU.is_equal, ["tA0", "tA1"], ["ma"], 256, c=0.5)
+
+    win = T.tab[:, 0:V]
+    nabs = [0]
+    for t in range(RO):
+        bias[0] = 0.0
+        A = T.tab[:, 128 * t:128 * t + 128]
+        kA = "tA%d" % t
+        p = pk[t]
+        k = "pk%d" % t
+        act(p[:, 128:256], T.tab[:, H:V].indirect(T.offb[:, 8 * t:8 * t + 8]), ACT.Copy, ["thi", "offb"], [k + "b"], 128, c=GA)
+        tt(T.d1[:], p[:, 128:256], T.ma[:, 128 * t:128 * t + 128], ALU.mult, [k + "b", "ma"], ["d1"], 128)
+        tt(p[:, 0:128], T.d1[:], A, ALU.add, ["d1", kA], [k + "a"], 128)
+        send("B%d" % t, judge[t], lb[t][:], p[:], [k + "a", k + "b"], ["lb%d" % t], None, 3000)
+        tt(T.daf[:, 128 * t:128 * t + 128], T.d1[:], T.fst[:, 128 * t:128 * t + 128], ALU.mult, ["d1", "fst%d" % t], ["daf%d" % t], 128)
+        kb = "lb%d" % t
+        for j in range(2):
+            r0 = 512 * j
+            act(T.rep[:, r0:r0 + 128], lb[t][:, 128 * j:128 * j + 128], ACT.Copy, [kb], ["repa%d" % j], 128)
+            act(T.rep[:, r0 + 128:r0 + 256], lb[t][:, 128 * j:128 * j + 128], ACT.Copy, [kb], ["repb%d" % j], 128)
+            act(T.rep[:, r0 + 256:r0 + 512], T.rep[:, r0:r0 + 256], ACT.Copy, ["repa%d" % j, "repb%d" % j], ["repc%d" % j], 256)
+        tile = [arep[t][:, 0:512], T.rep[:, 0:512], T.rep[:, 512:1024]]
+        tk = [RA[t], ["repa0", "repb0", "repc0"], ["repa1", "repb1", "repc1"]]
+        for j in range(3):
+            act(T.msk[:, 512 * j:512 * j + 512], tile[j], ACT.Relu, tk[j], ["msk%d" % j], 512, scale=-1.0, bias=1.0)
+
+        def steps(c):
+            m0, n = CH[c]
+            sg_ = sig[c]
+            C, P, J, c0, W = 128 * n, 128 * n // sg_, 8 * n, 128 * m0, 8 * sg_
+            us = list(range(m0 // 4, (m0 + n) // 4))
+            ko = "off%d" % c
+            bank, hn = reg[c]
+            hy = hn + W
+            for d in range(S):
+                n0 = V * d
+                step = 512 if d == 0 else min(GS, C)
+                for x0 in range(c0, c0 + C, step):
+                    uu = list(range(x0 // 512, (x0 + step) // 512))
+                    kn = ["n%d%d" % (d, u) for u in uu]
+                    nn = T.nb[:, n0 + x0:n0 + x0 + step]
+                    if d == 0:
+                        src = win.indirect(o0[t][:, x0 // 16:(x0 + step) // 16])
+                        if G0ENG[uu[0]] == "dve":
+                            cp(nn, src, TAB + ["o0%d%d" % (t, c)], kn, step, c=GA)
+                        else:
+                            act(nn, src, ACT.Copy, TAB + ["o0%d%d" % (t, c)], kn, step, c=GA)
+                    else:
+                        tt(nn, win.indirect(T.off[:, x0 // 16:(x0 + step) // 16]), T.yb[:, x0:x0 + step], ALU.min,
+                           TAB + [ko] + ["y%d" % u for u in uu], kn, step, c=GA)
+                if d == S - 1:
+                    if c == 0:
+                        act(T.don[:], win.indirect(T.off[:, 0:8]), ACT.Copy, TAB + [ko], ["don"], 128, c=GA)
+                        tt(ret[t][:, 0:128], T.don[:], lb[t][:, 128:256], ALU.subtract, ["don", kb], ["ret%da" % t], 128)
+                    break
+                kn = ["n%d%d" % (d, u) for u in us]
+                for u in us:
+                    kl, col = lease()
+                    o = ps[:, col:col + 512]
+                    lst = [(o, T.ineg[:], T.nb[:, n0 + 512 * u:n0 + 512 * u + 512], True, False, 512)]
+                    if d == 0:
+                        lst += [(ps[:, col + 128 * i:col + 128 * i + 128], T.i256[:], ah[t][:], False, i == 3, 128) for i in range(4)]
+                        mm(lst, ["n%d%d" % (d, u), "ineg", "i256", "ah%d" % t], [kl])
+                    else:
+                        lst += [(o, T.ident[:], T.yb[:, 512 * u:512 * u + 512], False, True, 512)]
+                        mm(lst, ["n%d%d" % (d, u), "ineg", "ident", "y%d" % u], [kl])
+                    act(T.yb[:, 512 * u:512 * u + 512], o, ACT.Relu, [kl], ["y%d" % u, kl], 512)
+                mm([(ps[0:P, hn + s:hn + W:sg_], T.nb[:, n0 + c0 + s:n0 + c0 + C:sg_], T.w8[:, 0:8], True, True, 64) for s in range(sg_)],
+                   kn + ["w8a"], ["hn%d" % c], [bank])
+                cs = T.cs[0:P, 128 * c:128 * c + W]
+                if d == 0:
+                    act(cs, ps[0:P, hn:hn + W], ACT.Copy, ["hn%d" % c], ["cs%d" % c], W, banks=[bank])
+                else:
+                    tt(cs, ps[0:P, hn:hn + W], cs, ALU.add, ["hn%d" % c, "cs%d" % c], ["cs%d" % c], W, banks=[bank], c=1.0)
+                mm([(ps[0:P, hy + s:hy + W:sg_], T.yb[:, c0 + s:c0 + C:sg_], T.w8[:, 8:16], True, True, 64) for s in range(sg_)],
+                   ["y%d" % u for u in us] + ["w8b"], ["hy%d" % c], [bank])
+                xi = T.xi[0:P, 128 * c:128 * c + W]
+                tt(xi, ps[0:P, hy:hy + W], cs, ALU.add, ["hy%d" % c, "cs%d" % c], ["xi%d" % c], W, banks=[bank], c=1.0)
+                ts(xi, xi, V - 1, ALU.bitwise_and, ["xi%d" % c], ["xi%d" % c], W)
+                chain(c, d + 1, xi, "xi%d" % c, c, hy, "hy%d" % c, [bank], T.off, ko)
+                if CDMA and d >= 1:
+                    k0 = ["n0%d" % u for u in us]
+                    add("pool", [lambda d=d: g.dma_start(T.nb[:, c0:c0 + C], T.nb[:, V * d + c0:V * d + c0 + C], accum_op=ALU.add)],
+                        1000, kn + k0, k0, kind="d", sem="ad%d%d%d" % (t, c, d), cnt=16, lat=2000 + 2.0 * C)
+                if t == 0 and c == 0 and d == 1:
+                    dma("sp", T.y[:, 256:H], T.tab[:, 256:H], ["tlo"] + kn, [], "ylo", 5000)
+
+        def verdict(u):
+            kl, col = lease()
+            o = ps[:, col:col + 512]
+            ds = [0, S - 1] if CDMA else list(range(S))
+            mm([(o, T.ident[:], T.nb[:, V * d + 512 * u:V * d + 512 * u + 512], d == 0, d == S - 1, 512) for d in ds],
+               ["n%d%d" % (d, u) for d in ds] + ["ident"], [kl])
+            for j in range(3):
+                tt(T.xs[:, V * j + 512 * u:V * j + 512 * u + 512], o, T.msk[:, 512 * j:512 * j + 512], ALU.mult,
+                   [kl, "msk%d" % j], ["x%d%d" % (j, u), kl], 512, c=1.0)
+            st = nabs[0] % 3
+            for j in range(3):
+                kl, col = lease()
+                o = ps[:, col:col + 512]
+                ka = "ab%d%d" % (st, j)
+                mm([(o, T.qblk[:], tile[j], True, False, 512), (o, T.qblk[:], T.xs[:, V * j + 512 * u:V * j + 512 * u + 512], False, True, 512)],
+                   QB + tk[j] + ["x%d%d" % (j, u)], [kl, ka])
+                a0 = 512 * (3 * st + j)
+                act(T.ab[:, a0:a0 + 512], o, ACT.Abs, [kl, "negt"], [ka, kl], 512, bias=T.negt[:, 0:1])
+            r = nabs[0] % 2
+            dq = 3968 + 64 * r
+            for q in range(4):
+                o = ps[:, dq + q:dq + 64:4]
+                a0 = 512 * 3 * st + 128 * q
+                mm([(o, T.ab[:, a0 + 512:a0 + 640], T.ob[:, 0:16], True, False, 256),
+                    (o, T.ab[:, a0:a0 + 128], T.ob[:, 16:32], False, False, 256),
+                    (o, T.ab[:, a0 + 1024:a0 + 1152], T.ob[:, 24:40], False, True, 256)],
+                   OB + ["ab%d%d" % (st, j) for j in range(3)], ["dq%d%d" % (r, q)], [7])
+            w = T.wg[:, 64 * r:64 * r + 64]
+            ts(w, ps[:, dq:dq + 64], 0.5, ALU.is_gt, ["dq%d%d" % (r, q) for q in range(4)], ["wg%d" % r], 64, banks=[7])
+            hf, mo = u // 4, 4 * (u % 4)
+            tt(T.worse[:, 8 * hf:8 * hf + 8, mo:mo + 4], T.wg[:, 64 * r:64 * r + 32], T.wg[:, 64 * r + 32:64 * r + 64], ALU.max,
+               ["wg%d" % r], ["worse%d" % u], 32)
+            nabs[0] += 1
+            if u % 4 == 3:
+                kl, col = lease()
+                o = ps[:, col:col + 128]
+                mm([(o, T.worse[:, 8 * hf:8 * hf + 8, :], T.ident[:], True, True, 128)], ["worse%d" % (4 * hf + i) for i in range(4)] + ["ident"], [kl])
+                act(T.wt[:, 128 * hf:128 * hf + 128], o, ACT.Copy, [kl], ["wt%d" % hf, kl], 128)
+
+        for c in range(nch):
+            bias[0] = BIAS[c]
+            steps(c)
+        bias[0] = 0.0
+        if t + 1 < RO:
+            RA.append(step0(t + 1))
+        for u in range(8):
+            bias[0] = VB + [BIAS[c] for c in range(nch) if CH[c][0] <= 4 * u][-1]
+            verdict(u)
+        bias[0] = 0.0
+        kl, col = lease()
+        o = ps[:, col:col + 128]
+        mm([(o, T.b16[:], T.wt[:, 0:128], True, False, 128), (o, T.b16[:], T.wt[:, 128:256], False, True, 128)], ["b16", "wt0", "wt1"], [kl])
+        cp(ret[t][:, 128:256], o, [kl], ["ret%db" % t, kl], 128)
+        send("R%d" % t, home[t], lr[t][:], ret[t][:], ["ret%da" % t, "ret%db" % t], ["lr%d" % t], None, 2500)
+        kr = "lr%d" % t
+        tt(T.fz[:], lr[t][:, 128:256], T.thr[:, 128 * t:128 * t + 128], ALU.is_le, [kr, "thr"], ["fz"], 128)
+        tt(T.tb[:], T.fz[:], lr[t][:, 0:128], ALU.mult, [kr, "fz"], ["tb"], 128)
+        tt(T.tab[:, H:V + L].indirect(T.offs[:, 8 * t:8 * t + 8]), T.tb[:], p[:, 128:256], ALU.add, ["tb", k + "b", "offs"], ["thi"], 128, c=4.0)
+        tt(T.ta[:], T.fz[:], T.daf[:, 128 * t:128 * t + 128], ALU.mult, ["fz", "daf%d" % t], ["ta"], 128)
+        tt(A, T.ta[:], A, ALU.add, ["ta", kA], [kA], 128)
+        dma("act" if t else "sp", T.y[:, 128 * t:128 * t + 128], A, [kA], [], "yA%d" % t, 2500)
+    dma("sp", T.y[:, H:V], T.tab[:, H:V], ["thi"], [], "yhi", 5000)
+    return ops
+
+
+def order(ops):
+    n = len(ops)
+    lastw, readers, first, last = {}, {}, {}, {}
+    deps = [dict() for _ in range(n)]
+    for i, o in enumerate(ops):
+        for k in o["r"]:
+            if k in lastw:
+                j, via = lastw[k]
+                deps[i][j] = via if deps[i].get(j) != "r" else "r"
+        for k in o["w"] + o["land"]:
+            if k in lastw:
+                deps[i].setdefault(lastw[k][0], lastw[k][1])
+            for j in readers.get(k, ()):
+                if j != i:
+                    deps[i].setdefault(j, "s")
+            if k[0] == "L":
+                first.setdefault(k, i)
+                last[k] = i
+        for k in o["r"]:
+            readers.setdefault(k, []).append(i)
+        for k in o["w"]:
+            lastw[k] = (i, "s")
+            readers[k] = []
+        for k in o["land"]:
+            lastw[k] = (i, "r")
+            readers[k] = []
+    acq = {i: k for k, i in first.items()}
+    rel = {i: k for k, i in last.items()}
+    succ = [[] for _ in range(n)]
+    for i in range(n):
+        for j in deps[i]:
+            succ[j].append(i)
+    pr = [0.0] * n
+    for i in range(n - 1, -1, -1):
+        pr[i] = ops[i]["dur"] + ops[i]["lat"] + max([pr[j] + HOP for j in succ[i]] + [0.0])
+    left = [len(d) for d in deps]
+    ready = [i for i in range(n) if left[i] == 0]
+    fin, free, blast, seq, assign = [0.0] * n, {}, {}, [], {}
+    spare = {b: None for b in range(6)}
+
+    def when(b):
+        return 0.0 if spare[b] is None else fin[spare[b]] + HOP
+
+    def start(i):
+        o = ops[i]
+        s = free.get(o["eng"], 0.0)
+        for j in deps[i]:
+            if not (o["eng"] == "pe" and ops[j]["eng"] == "pe"):
+                s = max(s, fin[j] + HOP)
+        for b in o["banks"]:
+            for e, j in blast.get(b, {}).items():
+                if e != o["eng"]:
+                    s = max(s, fin[j] + HOP)
+        if i in acq:
+            s = max(s, min(when(b) for b in spare))
+        return s
+    while ready:
+        st = [(start(i), i) for i in ready if spare or i not in acq]
+        lo = min(st)[0]
+        s, i = max([x for x in st if x[0] <= lo + WINDOW], key=lambda x: (pr[x[1]] + ops[x[1]]["bias"], -x[1]))
+        o = ops[i]
+        for b in o["banks"]:
+            for e, j in blast.get(b, {}).items():
+                if e != o["eng"]:
+                    deps[i].setdefault(j, "s")
+            blast.setdefault(b, {})[o["eng"]] = i
+        if i in acq:
+            b = min(spare, key=when)
+            if spare[b] is not None:
+                deps[i].setdefault(spare[b], "s")
+            del spare[b]
+            assign[acq[i]] = b
+        free[o["eng"]] = s + o["dur"]
+        fin[i] = s + o["dur"] + o["lat"]
+        if i in rel:
+            spare[assign[rel[i]]] = i
+        o["t0"] = s
+        seq.append(i)
+        ready.remove(i)
+        for j in succ[i]:
+            left[j] -= 1
+            if left[j] == 0:
+                ready.append(j)
+    return seq, deps, assign, max(fin)
+
+
+def rank_program(g, core, T, topo):
+    if T.rank_of(core) is None:
+        return
+    seq, deps, assign, _ = order(build(g, core, T, topo, {}))
+    ops = build(g, core, T, topo, assign)
+    Q = {"pe": g.tensor, "dve": g.vector, "act": g.scalar, "pool": g, "sp": g.sync}
+    count, mark, waited = {}, {}, {}
+    for i in seq:
+        o = ops[i]
+        e = o["eng"]
+        need = {}
+        for j, via in deps[i].items():
+            p = ops[j]
+            if p["kind"] == "c":
+                if e == "pe" and p["eng"] == "pe":
+                    continue
+                s, v = "c" + p["eng"], mark[j]
+            elif p["kind"] == "d":
+                s, v = p["sem"], 16
+            else:
+                s, v = via + p["sem"], p["cnt"]
+            need[s] = max(need.get(s, 0), v)
+        for s, v in need.items():
+            if waited.get((e, s), 0) < v:
+                Q[e].wait_ge(T.sem[s], v)
+                waited[(e, s)] = v
+        for fn in o["fns"]:
+            ins = fn()
+            if o["kind"] == "c":
+                ins.then_inc(T.sem["c" + e], 1)
+                count[e] = count.get(e, 0) + 1
+            elif o["kind"] == "d":
+                ins.then_inc(T.sem[o["sem"]], 16)
+        mark[i] = count.get(e, 0)
+    for e, v in count.items():
+        g.wait_ge(T.sem["c" + e], v)
+    for o in ops:
+        if o["kind"] == "r":
+            g.wait_ge(T.sem["s" + o["sem"]], o["cnt"])
+            g.wait_ge(T.sem["r" + o["sem"]], o["cnt"])
+    for o in ops:
+        if o["kind"] == "d":
+            g.wait_ge(T.sem[o["sem"]], 16)

@@ -6,14 +6,22 @@ ACT = ActivationFunctionType
 N, V, L, RO, S = 8, 4096, 128, 2, 6
 H = V // 2
 CH = [(0, 8), (8, 8), (16, 16)]
-BIAS = [13000.0, 4000.0, 2000.0, 0.0]
-G0ENG = ["dve", "act"] * 4
+BIAS = [14500.0, 6500.0, -500.0]
+G0ENG = ["dve", "act", "dve", "dve", "act", "act", "dve", "act"]
 GS = 512
-CDMA = True
+NADD = 3
+DQ = 1000.0
 DELTA = 12.5 / 32
-CY, PCY, HOP, GA, WINDOW = 1.04, 0.52, 110.0, 1.56, 30.0
-NC = 4
-VB = 0.0
+CY, PCY, HOP, GA, WINDOW = 1.04, 0.52, 220.0, 1.8, 30.0
+NC = 6
+UB = [-4000.0, 16000.0, -22000.0, -35000.0, 8000.0, 41000.0, 16000.0, 30000.0]
+SB = [5500.0, -9000.0, 1500.0, 10500.0, 12000.0, -15000.0]
+VB = -3000.0
+XDMA = 0
+XACT = 0
+MOD1 = False
+CSA = False
+M12 = 1.5 * 2.0 ** 35
 
 BF, F32, I32, U16 = "bfloat16", "float32", "int32", "uint16"
 SCRATCH = {
@@ -47,19 +55,22 @@ SCRATCH = {
     "lr0": ("sbuf", [128, 256], BF), "lr1": ("sbuf", [128, 256], BF),
     "arep0": ("sbuf", [128, 2048], BF), "arep1": ("sbuf", [128, 2048], BF),
     "ah0": ("sbuf", [128, 128], BF), "ah1": ("sbuf", [128, 128], BF), "aht": ("sbuf", [128, 128], BF),
-    "rep": ("sbuf", [128, 1024], BF), "msk": ("sbuf", [128, 1536], BF),
-    "nb": ("sbuf", [128, S * V], BF), "yb": ("sbuf", [128, V], BF), "xs": ("sbuf", [128, 3 * V], BF),
+    "rep": ("sbuf", [128, 3, 512], BF), "msk": ("sbuf", [128, 1536], BF), "rr": ("sbuf", [128, 128 * NC], F32),
+    "i256n": ("sbuf", [128, 128], BF), "acol2": ("sbuf", [128, NC], F32),
+    "nb": ("sbuf", [128, S * V], BF), "yb": ("sbuf", [128, V], BF), "xs": ("sbuf", [128, 3, V], BF),
     "ab": ("sbuf", [128, 9 * 512], F32),
     "cs": ("sbuf", [128, 128 * NC], F32), "xi": ("sbuf", [128, 256 * NC], I32), "vf": ("sbuf", [128, 256 * NC], F32),
-    "v8": ("sbuf", [128, 64], I32), "v16": ("sbuf", [128, 128], I32), "hf": ("sbuf", [128, 256 * NC], F32),
-    "pad": ("sbuf", [128, 2 * NC * 17, 8], F32), "off": ("sbuf", [128, 256], U16),
+    "v8": ("sbuf", [128, 64], I32), "v16": ("sbuf", [128, 128], I32), "hf": ("sbuf", [128, 256 * NC], "float16"),
+    "selh": ("sbuf", [128, 128], "float16"), "identh": ("sbuf", [128, 128], "float16"),
+    "pad": ("sbuf", [128, 2 * NC * 17, 8], "float16"), "off": ("sbuf", [128, 256], U16),
     "o00": ("sbuf", [128, 256], U16), "o01": ("sbuf", [128, 256], U16),
     "wg": ("sbuf", [128, 128], BF), "worse": ("sbuf", [128, 16, 16], BF), "wt": ("sbuf", [128, 256], BF),
     "don": ("sbuf", [128, 128], BF), "fz": ("sbuf", [128, 128], BF), "ta": ("sbuf", [128, 128], BF),
     "tb": ("sbuf", [128, 128], BF),
 }
 DMAS = ["lA", "lhw", "lhi", "llo", "lgo", "lmx", "ylo", "yA0", "yA1", "yhi"]
-ADDS = ["ad%d%d%d" % (t, c, d) for t in range(RO) for c in range(len(CH)) for d in range(1, S - 1)] if CDMA else []
+ADDS = ["ad%d%d%d" % (t, c, d) for t in range(RO) for c in range(len(CH)) for d in range(1, NADD + 1)]
+ADDS += ["ax%d%d" % (t, u) for t in range(RO) for u in range(XDMA)]
 REMS = ["A0", "A1", "B0", "B1", "R0", "R1"]
 SEMAPHORES = ["cpe", "cdve", "cact", "cpool"] + DMAS + ADDS + ["r" + n for n in REMS] + ["s" + n for n in REMS]
 
@@ -152,11 +163,14 @@ def build(g, core, T, topo, assign):
     pool(lambda: g.iota(T.pi[:, 0:1], [[0, 1]], 0, 1), 1, [], ["pi"])
     if 8 in sig:
         pool(lambda: g.affine_select(T.sel[:], T.onef[:], [[-1, 2], [-2, 64]], ALU.is_equal, 0.0, 0, 1), 128, ["onef"], ["sel"])
+        cp(T.selh[:], T.sel[:], ["sel"], ["selh"], 128)
         for c in range(nch):
             if sig[c] == 8:
-                for tmp in (c, NC + c):
-                    ms(T.pad[:, 17 * tmp:17 * tmp + 17, :], 0.0, ["pad%d" % tmp], 272)
+                for tmp in (NC + c, c):
+                    ts(T.pad[:, 17 * tmp:17 * tmp + 17:2, :], T.ones[:, 0:72], 0.0, ALU.mult, ["ones"], ["pad%d" % tmp], 72, c=0.5)
     pool(lambda: g.affine_select(T.identf[:], T.onef[:], [[-1, 128]], ALU.is_equal, 0.0, 0, 1), 128, ["onef"], ["identf"])
+    if 16 in sig:
+        cp(T.identh[:], T.identf[:], ["identf"], ["identh"], 128)
     send("A0", judge[0], la[0][:], T.tab[:, 0:128], ["tA0"], ["la0"], 0, 3500)
     pool(lambda: g.iota(T.mi[:], [[-1, 256]], 256, 1), 256, [], ["mi"])
     send("A1", judge[1], la[1][:], T.tab[:, 128:256], ["tA1"], ["la1"], 1, 3500)
@@ -175,6 +189,9 @@ def build(g, core, T, topo, assign):
         ts(T.mo[:, c:c + 1], T.pi[:, j:j + 1], 2.0, ALU.mult, ["pi%d" % j], ["mo%d" % c], 1, 2.0 * CH[c][0] + 1, ALU.add)
     MO = ["mo%d" % c for c in range(nch)]
     act(T.acol[:, 0:nch], T.mo[:, 0:nch], ACT.Copy, MO, ["acol"], nch, scale=16.0)
+    act(T.acol2[:, 0:nch], T.mo[:, 0:nch], ACT.Identity, MO, ["acol2"], nch, scale=16.0, bias=2048.0)
+    if XACT:
+        act(T.i256n[:], T.identf[:], ACT.Copy, ["identf"], ["i256n"], 128, scale=-256.0)
     act(T.k0[:, 0:nch], T.mo[:, 0:nch], ACT.Square, MO, ["k0"], nch)
     for d in range(S):
         act(T.kcol[:, NC * d:NC * d + nch], T.k0[:, 0:nch], ACT.Identity, ["k0"], ["kcol%d" % d], nch, scale=-8.0, bias=811.0 * d - DELTA)
@@ -201,21 +218,24 @@ def build(g, core, T, topo, assign):
         P = 128 * n // sig[c]
         xi, vf = T.xi[0:P, 128 * tmp:128 * tmp + W], T.vf[0:P, 128 * tmp:128 * tmp + W]
         kx, kv, kp = "xi%d" % tmp, "vf%d" % tmp, "pad%d" % tmp
-        ts(vf, src, T.acol[0:P, c:c + 1], ALU.add, [srck, "acol"], [kv], W)
-        act(vf, vf, ACT.Square, [kv], [kv], W)
+        if src is None:
+            act(vf, vf, ACT.Square, [kv, "acol2"], [kv], W, bias=T.acol2[0:P, c:c + 1])
+        else:
+            ts(vf, src, T.acol[0:P, c:c + 1], ALU.add, [srck, "acol"], [kv], W)
+            act(vf, vf, ACT.Square, [kv], [kv], W)
         ts(xi, vf, 1.0 / 32, ALU.mult, [kv, "kcol%d" % d], [kx], W, T.kcol[0:P, NC * d + c:NC * d + c + 1], ALU.add)
         ts(xi, xi, V - 1, ALU.bitwise_and, [kx], [kx], W)
         tr = ps[:, col:col + J]
         if sig[c] == 8:
             b = 17 * tmp
-            cp(T.pad[0:P, b + 1:b + 17:2, :], xi, [kx], [kp], W)
-            mm([(tr, T.pad[0:P, b + 1:b + 17, :], T.sel[0:P, 0:J], True, False, 256),
-                (tr, T.pad[0:P, b:b + 16, :], T.sel[0:P, 64:64 + J], False, True, 256)], [kp, "sel"], [kt], banks)
+            ts(T.pad[0:P, b + 1:b + 17:2, :], xi, -2048.0, ALU.add, [kx], [kp], W)
+            mm([(tr, T.pad[0:P, b + 1:b + 17, :], T.selh[0:P, 0:J], True, False, 64),
+                (tr, T.pad[0:P, b:b + 16, :], T.selh[0:P, 64:64 + J], False, True, 64)], [kp, "selh"], [kt], banks)
         else:
             hf = T.hf[:, 128 * tmp:128 * tmp + 128]
-            cp(hf, xi, [kx], [kp], W)
-            mm([(tr, hf, T.identf[:], True, True, 512)], [kp, "identf"], [kt], banks)
-        cp(dst[:, 8 * m0:8 * m0 + J], tr, [kt], [dstk, kt], J, banks=banks)
+            ts(hf, xi, -2048.0, ALU.add, [kx], [kp], W)
+            mm([(tr, hf, T.identh[:], True, True, 128)], [kp, "identh"], [kt], banks)
+        ts(dst[:, 8 * m0:8 * m0 + J], tr, 2048.0, ALU.add, [kt], [dstk, kt], J, banks=banks)
 
     def step0(t):
         a, r = la[t], arep[t]
@@ -278,7 +298,7 @@ def build(g, core, T, topo, assign):
     add("dve", [lambda: ve.tensor_tensor_scan(T.t2[:], T.rst[:], T.t1[:], 0.0, ALU.mult, ALU.add)], vd(256), ["t1", "rst"], ["t2"])
     cp(T.offb[:], T.t2[:, 15:256:16], ["t2"], ["offb"], 16)
     ts(T.upar[:], T.ui[:], 1, ALU.bitwise_and, ["ui"], ["upar"], 256)
-    ts(T.thr[:], T.upar[:], 20.5, ALU.add, ["upar"], ["thr"], 256)
+    ts(T.thr[:], T.upar[:], 2.0, ALU.mult, ["upar"], ["thr"], 256, 9.0, ALU.add)
     tt(T.t3[:], T.bfl[:], T.dump[:], ALU.subtract, ["bfl", "dump"], ["t3"], 256)
     tt(T.t3[:], T.t3[:], T.fst[:], ALU.mult, ["t3", "fst0", "fst1"], ["t3"], 256)
     tt(T.t3[:], T.t3[:], T.dump[:], ALU.add, ["t3", "dump"], ["t3"], 256)
@@ -301,13 +321,13 @@ def build(g, core, T, topo, assign):
         send("B%d" % t, judge[t], lb[t][:], p[:], [k + "a", k + "b"], ["lb%d" % t], None, 3000)
         tt(T.daf[:, 128 * t:128 * t + 128], T.d1[:], T.fst[:, 128 * t:128 * t + 128], ALU.mult, ["d1", "fst%d" % t], ["daf%d" % t], 128)
         kb = "lb%d" % t
+        act(T.rep[:, 0, :], arep[t][:, 0:512], ACT.Copy, RA[t], ["repA"], 512)
         for j in range(2):
-            r0 = 512 * j
-            act(T.rep[:, r0:r0 + 128], lb[t][:, 128 * j:128 * j + 128], ACT.Copy, [kb], ["repa%d" % j], 128)
-            act(T.rep[:, r0 + 128:r0 + 256], lb[t][:, 128 * j:128 * j + 128], ACT.Copy, [kb], ["repb%d" % j], 128)
-            act(T.rep[:, r0 + 256:r0 + 512], T.rep[:, r0:r0 + 256], ACT.Copy, ["repa%d" % j, "repb%d" % j], ["repc%d" % j], 256)
-        tile = [arep[t][:, 0:512], T.rep[:, 0:512], T.rep[:, 512:1024]]
-        tk = [RA[t], ["repa0", "repb0", "repc0"], ["repa1", "repb1", "repc1"]]
+            act(T.rep[:, j + 1, 0:128], lb[t][:, 128 * j:128 * j + 128], ACT.Copy, [kb], ["repa%d" % j], 128)
+            act(T.rep[:, j + 1, 128:256], lb[t][:, 128 * j:128 * j + 128], ACT.Copy, [kb], ["repb%d" % j], 128)
+            act(T.rep[:, j + 1, 256:512], T.rep[:, j + 1, 0:256], ACT.Copy, ["repa%d" % j, "repb%d" % j], ["repc%d" % j], 256)
+        tile = [T.rep[:, j, :] for j in range(3)]
+        tk = [["repA"], ["repa0", "repb0", "repc0"], ["repa1", "repb1", "repc1"]]
         for j in range(3):
             act(T.msk[:, 512 * j:512 * j + 512], tile[j], ACT.Relu, tk[j], ["msk%d" % j], 512, scale=-1.0, bias=1.0)
 
@@ -321,6 +341,7 @@ def build(g, core, T, topo, assign):
             hy = hn + W
             for d in range(S):
                 n0 = V * d
+                bias[0] = BIAS[c] + SB[d]
                 step = 512 if d == 0 else min(GS, C)
                 for x0 in range(c0, c0 + C, step):
                     uu = list(range(x0 // 512, (x0 + step) // 512))
@@ -352,41 +373,64 @@ def build(g, core, T, topo, assign):
                         lst += [(o, T.ident[:], T.yb[:, 512 * u:512 * u + 512], False, True, 512)]
                         mm(lst, ["n%d%d" % (d, u), "ineg", "ident", "y%d" % u], [kl])
                     act(T.yb[:, 512 * u:512 * u + 512], o, ACT.Relu, [kl], ["y%d" % u, kl], 512)
-                mm([(ps[0:P, hn + s:hn + W:sg_], T.nb[:, n0 + c0 + s:n0 + c0 + C:sg_], T.w8[:, 0:8], True, True, 64) for s in range(sg_)],
-                   kn + ["w8a"], ["hn%d" % c], [bank])
                 cs = T.cs[0:P, 128 * c:128 * c + W]
-                if d == 0:
-                    act(cs, ps[0:P, hn:hn + W], ACT.Copy, ["hn%d" % c], ["cs%d" % c], W, banks=[bank])
+                car = CSA and d > 0
+                mm([(ps[0:P, hn:hn + W], T.identf[0:P, 0:P], cs, True, False, 4 * W)] * car +
+                   [(ps[0:P, hn + s:hn + W:sg_], T.nb[:, n0 + c0 + s:n0 + c0 + C:sg_], T.w8[:, 0:8], not car, s == sg_ - 1 or not car, 64)
+                    for s in range(sg_)], kn + ["w8a", "identf"] + ["cs%d" % c] * car, ["hn%d" % c], [bank])
+                if d == 0 or CSA:
+                    act(cs, ps[0:P, hn:hn + W], ACT.Identity, ["hn%d" % c], ["cs%d" % c], W, banks=[bank],
+                        bias=-2048.0 if MOD1 and d == 0 else 0.0)
                 else:
                     tt(cs, ps[0:P, hn:hn + W], cs, ALU.add, ["hn%d" % c, "cs%d" % c], ["cs%d" % c], W, banks=[bank], c=1.0)
                 mm([(ps[0:P, hy + s:hy + W:sg_], T.yb[:, c0 + s:c0 + C:sg_], T.w8[:, 8:16], True, True, 64) for s in range(sg_)],
                    ["y%d" % u for u in us] + ["w8b"], ["hy%d" % c], [bank])
                 xi = T.xi[0:P, 128 * c:128 * c + W]
-                tt(xi, ps[0:P, hy:hy + W], cs, ALU.add, ["hy%d" % c, "cs%d" % c], ["xi%d" % c], W, banks=[bank], c=1.0)
-                ts(xi, xi, V - 1, ALU.bitwise_and, ["xi%d" % c], ["xi%d" % c], W)
-                chain(c, d + 1, xi, "xi%d" % c, c, hy, "hy%d" % c, [bank], T.off, ko)
-                if CDMA and d >= 1:
+                if MOD1:
+                    x, rr = ps[0:P, hy:hy + W], T.rr[0:P, 128 * c:128 * c + W]
+                    tt(x, x, cs, ALU.add, ["hy%d" % c, "cs%d" % c], ["hy%d" % c], W, banks=[bank], c=1.0)
+                    act(rr, x, ACT.Identity, ["hy%d" % c], ["rr%d" % c], W, banks=[bank], bias=M12)
+                    act(rr, rr, ACT.Identity, ["rr%d" % c], ["rr%d" % c], W, bias=-M12)
+                    tt(T.vf[0:P, 128 * c:128 * c + W], x, rr, ALU.subtract, ["hy%d" % c, "rr%d" % c], ["vf%d" % c], W, banks=[bank], c=1.0)
+                    chain(c, d + 1, None, None, c, hy, "hy%d" % c, [bank], T.off, ko)
+                else:
+                    tt(xi, ps[0:P, hy:hy + W], cs, ALU.add, ["hy%d" % c, "cs%d" % c], ["xi%d" % c], W, banks=[bank], c=1.0)
+                    ts(xi, xi, V - 1, ALU.bitwise_and, ["xi%d" % c], ["xi%d" % c], W)
+                    chain(c, d + 1, xi, "xi%d" % c, c, hy, "hy%d" % c, [bank], T.off, ko)
+                if 1 <= d <= NADD:
                     k0 = ["n0%d" % u for u in us]
                     add("pool", [lambda d=d: g.dma_start(T.nb[:, c0:c0 + C], T.nb[:, V * d + c0:V * d + c0 + C], accum_op=ALU.add)],
-                        1000, kn + k0, k0, kind="d", sem="ad%d%d%d" % (t, c, d), cnt=16, lat=2000 + 2.0 * C)
+                        DQ, kn + k0, k0, kind="d", sem="ad%d%d%d" % (t, c, d), cnt=16, lat=2000 + 2.0 * C)
                 if t == 0 and c == 0 and d == 1:
                     dma("sp", T.y[:, 256:H], T.tab[:, 256:H], ["tlo"] + kn, [], "ylo", 5000)
 
         def verdict(u):
             kl, col = lease()
             o = ps[:, col:col + 512]
-            ds = [0, S - 1] if CDMA else list(range(S))
+            ds = [0] + list(range(NADD + 1, S))
             mm([(o, T.ident[:], T.nb[:, V * d + 512 * u:V * d + 512 * u + 512], d == 0, d == S - 1, 512) for d in ds],
                ["n%d%d" % (d, u) for d in ds] + ["ident"], [kl])
-            for j in range(3):
-                tt(T.xs[:, V * j + 512 * u:V * j + 512 * u + 512], o, T.msk[:, 512 * j:512 * j + 512], ALU.mult,
+            xa = min(3, (XACT + 7 - u) // 8)
+            for j in range(xa, 3):
+                tt(T.xs[:, j, 512 * u:512 * u + 512], o, T.msk[:, 512 * j:512 * j + 512], ALU.mult,
                    [kl, "msk%d" % j], ["x%d%d" % (j, u), kl], 512, c=1.0)
+            for j in range(xa):
+                kl, col = lease()
+                o = ps[:, col:col + 512]
+                mm([(o, T.i256n[:], tile[j], True, False, 512)] +
+                   [(o, T.ident[:], T.nb[:, V * d + 512 * u:V * d + 512 * u + 512], False, d == S - 1, 512) for d in ds],
+                   ["n%d%d" % (d, u) for d in ds] + ["ident", "i256n"] + tk[j], [kl])
+                act(T.xs[:, j, 512 * u:512 * u + 512], o, ACT.Relu, [kl], ["x%d%d" % (j, u), kl], 512)
+            if u < XDMA:
+                kx = ["x%d%d" % (j, u) for j in range(3)]
+                add("pool", [lambda: g.dma_start(T.xs[:, :, 512 * u:512 * u + 512], T.rep[:], accum_op=ALU.add)],
+                    1000, kx + tk[0] + tk[1] + tk[2], kx, kind="d", sem="ax%d%d" % (t, u), cnt=16, lat=5000)
             st = nabs[0] % 3
             for j in range(3):
                 kl, col = lease()
                 o = ps[:, col:col + 512]
                 ka = "ab%d%d" % (st, j)
-                mm([(o, T.qblk[:], tile[j], True, False, 512), (o, T.qblk[:], T.xs[:, V * j + 512 * u:V * j + 512 * u + 512], False, True, 512)],
+                mm([(o, T.qblk[:], tile[j], True, False, 512)] * (u >= XDMA) + [(o, T.qblk[:], T.xs[:, j, 512 * u:512 * u + 512], u < XDMA, True, 512)],
                    QB + tk[j] + ["x%d%d" % (j, u)], [kl, ka])
                 a0 = 512 * (3 * st + j)
                 act(T.ab[:, a0:a0 + 512], o, ACT.Abs, [kl, "negt"], [ka, kl], 512, bias=T.negt[:, 0:1])
@@ -400,7 +444,7 @@ def build(g, core, T, topo, assign):
                     (o, T.ab[:, a0 + 1024:a0 + 1152], T.ob[:, 24:40], False, True, 256)],
                    OB + ["ab%d%d" % (st, j) for j in range(3)], ["dq%d%d" % (r, q)], [7])
             w = T.wg[:, 64 * r:64 * r + 64]
-            ts(w, ps[:, dq:dq + 64], 0.5, ALU.is_gt, ["dq%d%d" % (r, q) for q in range(4)], ["wg%d" % r], 64, banks=[7])
+            act(w, ps[:, dq:dq + 64], ACT.Sign, ["dq%d%d" % (r, q) for q in range(4)], ["wg%d" % r], 64, banks=[7], bias=-0.5)
             hf, mo = u // 4, 4 * (u % 4)
             tt(T.worse[:, 8 * hf:8 * hf + 8, mo:mo + 4], T.wg[:, 64 * r:64 * r + 32], T.wg[:, 64 * r + 32:64 * r + 64], ALU.max,
                ["wg%d" % r], ["worse%d" % u], 32)
@@ -418,7 +462,7 @@ def build(g, core, T, topo, assign):
         if t + 1 < RO:
             RA.append(step0(t + 1))
         for u in range(8):
-            bias[0] = VB + [BIAS[c] for c in range(nch) if CH[c][0] <= 4 * u][-1]
+            bias[0] = VB + UB[u] + [BIAS[c] for c in range(nch) if CH[c][0] <= 4 * u][-1]
             verdict(u)
         bias[0] = 0.0
         kl, col = lease()

from concourse.bass import DstId, RemoteDMATransfer
from concourse.mybir import dt, AluOpType, AxisListType, ActivationFunctionType

ALU = AluOpType
ACT = ActivationFunctionType
N, V, L, RO, S = 8, 4096, 128, 2, 6
H = V // 2
CH = [(0, 8), (8, 8), (16, 16)]
BIAS = [14500.0, 6500.0, -500.0]
G0ENG = ["dve", "act", "dve", "dve", "act", "act", "dve", "act"]
GS = 512
NADD = 3
DQ = 1000.0
DELTA = 12.5 / 32
CY, PCY, HOP, GA, WINDOW = 1.04, 0.52, 220.0, 1.8, 30.0
NC = 6
UB = [-4000.0, 16000.0, -22000.0, -35000.0, 8000.0, 41000.0, 16000.0, 30000.0]
SB = [5500.0, -9000.0, 1500.0, 10500.0, 12000.0, -15000.0]
VB = -3000.0
XDMA = 0
XACT = 0
MOD1 = False
CSA = False
M12 = 1.5 * 2.0 ** 35

BF, F32, I32, U16 = "bfloat16", "float32", "int32", "uint16"
SCRATCH = {
    "ps": ("psum", [128, 4096], F32),
    "tab": ("sbuf", [128, V + L], BF),
    "hwi": ("sbuf", [128, 4], I32), "goi": ("sbuf", [128, 4], I32), "mixs": ("sbuf", [128, 16], BF),
    "wf": ("sbuf", [128, 1], F32), "negt": ("sbuf", [128, 1], F32),
    "ones": ("sbuf", [128, 1024], BF), "onef": ("sbuf", [128, 128], F32),
    "ident": ("sbuf", [128, 128], BF), "identf": ("sbuf", [128, 128], F32),
    "i256": ("sbuf", [128, 128], BF), "ineg": ("sbuf", [128, 128], BF),
    "b16a": ("sbuf", [128, 128], BF), "b16": ("sbuf", [128, 128], BF), "bmf": ("sbuf", [128, 8], F32),
    "wblk": ("sbuf", [128, 128], BF), "w8": ("sbuf", [128, 16], BF), "qblk": ("sbuf", [128, 128], BF),
    "sel": ("sbuf", [128, 128], F32), "ob": ("sbuf", [128, 40], F32),
    "sg": ("sbuf", [128, 1024], BF), "big": ("sbuf", [128, 128], BF), "upp": ("sbuf", [128, 128], BF),
    "z2": ("sbuf", [128, 240], BF),
    "pi": ("sbuf", [128, 4], I32), "mo": ("sbuf", [128, NC], F32),
    "acol": ("sbuf", [128, NC], F32), "k0": ("sbuf", [128, NC], F32), "kcol": ("sbuf", [128, 6 * NC], F32),
    "mi": ("sbuf", [128, 256], I32), "m16": ("sbuf", [128, 256], F32), "rst": ("sbuf", [128, 256], F32),
    "dump": ("sbuf", [128, 256], F32),
    "ui": ("sbuf", [128, 256], I32), "upar": ("sbuf", [128, 256], I32), "thr": ("sbuf", [128, 256], BF),
    "uf": ("sbuf", [128, 256], F32), "bi": ("sbuf", [128, 256], I32), "bfl": ("sbuf", [128, 256], F32),
    "xy": ("sbuf", [128, 512], BF), "nxy": ("sbuf", [128, 512], BF), "t1": ("sbuf", [128, 256], F32),
    "t2": ("sbuf", [128, 256], F32), "t3": ("sbuf", [128, 256], F32), "t4": ("sbuf", [128, 256], F32),
    "offb": ("sbuf", [128, 16], U16), "offs": ("sbuf", [128, 16], U16),
    "eq": ("sbuf", [128, 2048], BF), "fst": ("sbuf", [128, 256], BF),
    "ma": ("sbuf", [128, 256], BF), "daf": ("sbuf", [128, 256], BF), "d1": ("sbuf", [128, 128], BF),
    "pk0": ("sbuf", [128, 256], BF), "pk1": ("sbuf", [128, 256], BF),
    "lb0": ("sbuf", [128, 256], BF), "lb1": ("sbuf", [128, 256], BF),
    "la0": ("sbuf", [128, 128], BF), "la1": ("sbuf", [128, 128], BF),
    "ret0": ("sbuf", [128, 256], BF), "ret1": ("sbuf", [128, 256], BF),
    "lr0": ("sbuf", [128, 256], BF), "lr1": ("sbuf", [128, 256], BF),
    "arep0": ("sbuf", [128, 2048], BF), "arep1": ("sbuf", [128, 2048], BF),
    "ah0": ("sbuf", [128, 128], BF), "ah1": ("sbuf", [128, 128], BF), "aht": ("sbuf", [128, 128], BF),
    "rep": ("sbuf", [128, 3, 512], BF), "msk": ("sbuf", [128, 1536], BF), "rr": ("sbuf", [128, 128 * NC], F32),
    "i256n": ("sbuf", [128, 128], BF), "acol2": ("sbuf", [128, NC], F32),
    "nb": ("sbuf", [128, S * V], BF), "yb": ("sbuf", [128, V], BF), "xs": ("sbuf", [128, 3, V], BF),
    "ab": ("sbuf", [128, 9 * 512], F32),
    "cs": ("sbuf", [128, 128 * NC], F32), "xi": ("sbuf", [128, 256 * NC], I32), "vf": ("sbuf", [128, 256 * NC], F32),
    "v8": ("sbuf", [128, 64], I32), "v16": ("sbuf", [128, 128], I32), "hf": ("sbuf", [128, 256 * NC], "float16"),
    "selh": ("sbuf", [128, 128], "float16"), "identh": ("sbuf", [128, 128], "float16"),
    "pad": ("sbuf", [128, 2 * NC * 17, 8], "float16"), "off": ("sbuf", [128, 256], U16),
    "o00": ("sbuf", [128, 256], U16), "o01": ("sbuf", [128, 256], U16),
    "wg": ("sbuf", [128, 128], BF), "worse": ("sbuf", [128, 16, 16], BF), "wt": ("sbuf", [128, 256], BF),
    "don": ("sbuf", [128, 128], BF), "fz": ("sbuf", [128, 128], BF), "ta": ("sbuf", [128, 128], BF),
    "tb": ("sbuf", [128, 128], BF),
}
DMAS = ["lA", "lhw", "lhi", "llo", "lgo", "lmx", "ylo", "yA0", "yA1", "yhi"]
ADDS = ["ad%d%d%d" % (t, c, d) for t in range(RO) for c in range(len(CH)) for d in range(1, NADD + 1)]
ADDS += ["ax%d%d" % (t, u) for t in range(RO) for u in range(XDMA)]
REMS = ["A0", "A1", "B0", "B1", "R0", "R1"]
SEMAPHORES = ["cpe", "cdve", "cact", "cpool"] + DMAS + ADDS + ["r" + n for n in REMS] + ["s" + n for n in REMS]


def build(g, core, T, topo, assign):
    rank = T.rank_of(core)
    ops = []
    ve, sc, pe = g.vector, g.scalar, g.tensor
    ps = T.ps
    bias, nl = [0.0], [0]

    def add(eng, fns, dur, r, w, banks=(), kind="c", sem=None, cnt=0, land=(), lat=0.0):
        ops.append(dict(eng=eng, fns=fns, dur=dur, r=list(r), w=list(w), banks=list(banks), kind=kind,
                        sem=sem, cnt=cnt, land=list(land), lat=lat, bias=bias[0]))

    def lease():
        nl[0] += 1
        k = "L%d" % nl[0]
        return k, 512 * assign.get(k, 0)

    def vd(n, c=1.0):
        return 40 + max(64, n * c) * CY

    def ts(out, in0, s1, op0, r, w, n, s2=None, op1=None, banks=(), c=1.0):
        if op1 is None:
            add("dve", [lambda: ve.tensor_scalar(out, in0, s1, None, op0)], vd(n, c), r, w, banks)
        else:
            add("dve", [lambda: ve.tensor_scalar(out, in0, s1, s2, op0, op1)], vd(n, c), r, w, banks)

    def tt(out, a, b, op, r, w, n, banks=(), c=2.0):
        add("dve", [lambda: ve.tensor_tensor(out, a, b, op)], vd(n, c), r, w, banks)

    def cp(out, a, r, w, n, banks=(), c=1.0):
        add("dve", [lambda: ve.tensor_copy(out, a)], vd(n, c), r, w, banks)

    def ms(out, val, w, n):
        add("dve", [lambda: ve.memset(out, val)], vd(n, 0.5), [], w)

    def act(out, a, f, r, w, n, banks=(), c=1.0, **kw):
        add("act", [lambda: sc.activation(out, a, f, **kw)], 60 + max(64, n * c) * CY, r, w, banks)

    def mm(lst, r, w, banks=()):
        fns, dur = [], 30.0
        for (o, l, x, st, sp, cyc) in lst:
            fns.append(lambda o=o, l=l, x=x, st=st, sp=sp: pe.matmul(o, l, x, st, sp))
            dur += cyc * PCY
        add("pe", fns, dur, r, w, banks)

    def dma(q, out, a, r, w, sem, lat):
        qq = g.sync if q == "sp" else sc
        add(q, [lambda: qq.dma_start(out, a)], 60, r, w, kind="d", sem=sem, cnt=16, lat=lat)

    def send(name, dst, out, a, r, land, part, lat):
        es = topo.engines(core, dst)[:8]
        es = es if part is None else es[part::2]
        m = 0
        for e in es:
            m |= 1 << e
        rid, pid, _ = topo.addr(dst)
        add("pool", [lambda: g.remote_dma(out, a, T.sem["r" + name], T.sem["s" + name], pid, rid, m)], 300, r, [],
            kind="r", sem=name, cnt=len(es), land=land, lat=lat)

    def pool(fn, n, r, w):
        add("pool", [fn], 170 + 2 * n * CY, r, w)

    TAB = ["tA0", "tA1", "tlo", "thi"]
    judge = [T.cores[(rank + 1 + t % (N - 1)) % N] for t in range(RO)]
    home = [T.cores[(rank - 1 - t % (N - 1)) % N] for t in range(RO)]
    la, lb, lr = [T.la0, T.la1], [T.lb0, T.lb1], [T.lr0, T.lr1]
    pk, ret, arep, ah, o0 = [T.pk0, T.pk1], [T.ret0, T.ret1], [T.arep0, T.arep1], [T.ah0, T.ah1], [T.o00, T.o01]
    sig = [16 if n == 16 else 8 for (_, n) in CH]
    nch = len(CH)
    reg, fill = [], [3072, 3584]
    for c in range(nch):
        b = c % 2 if fill[c % 2] + 16 * sig[c] <= (3584, 3968)[c % 2] else 1 - c % 2
        reg.append((6 + b, fill[b]))
        fill[b] += 16 * sig[c]

    dma("sp", T.tab[:, 0:256], T.ent[:, 0:256], [], ["tA0", "tA1"], "lA", 2300)
    dma("act", T.hwi[:, 0:1], T.hw[:], [], ["hwi"], "lhw", 2200)
    dma("sp", T.tab[:, H:V], T.ent[:, H:V], [], ["thi"], "lhi", 5000)
    dma("act", T.tab[:, 256:H], T.ent[:, 256:H], [], ["tlo"], "llo", 7000)
    dma("sp", T.goi[:, 0:1], T.goal[:], [], ["goi"], "lgo", 7000)
    dma("sp", T.mixs[:], T.mix[:], [], ["mixs"], "lmx", 7000)
    ms(T.ones[:, 0:128], 1.0, ["ones"], 128)
    ms(T.ones[:, 128:1024], 1.0, ["onesb"], 896)
    ms(T.onef[:], 1.0, ["onef"], 256)
    pool(lambda: g.affine_select(T.b16a[:], T.ones[:, 0:128], [[-16, 8], [0, 16]], ALU.is_ge, 0.0, 0, 1), 128, ["ones"], ["b16a"])
    pool(lambda: g.affine_select(T.b16[:], T.b16a[:], [[16, 8], [0, 16]], ALU.is_ge, 0.0, 15, -1), 128, ["b16a"], ["b16"])
    pool(lambda: g.iota(T.pi[:, 0:1], [[0, 1]], 0, 1), 1, [], ["pi"])
    if 8 in sig:
        pool(lambda: g.affine_select(T.sel[:], T.onef[:], [[-1, 2], [-2, 64]], ALU.is_equal, 0.0, 0, 1), 128, ["onef"], ["sel"])
        cp(T.selh[:], T.sel[:], ["sel"], ["selh"], 128)
        for c in range(nch):
            if sig[c] == 8:
                for tmp in (NC + c, c):
                    ts(T.pad[:, 17 * tmp:17 * tmp + 17:2, :], T.ones[:, 0:72], 0.0, ALU.mult, ["ones"], ["pad%d" % tmp], 72, c=0.5)
    pool(lambda: g.affine_select(T.identf[:], T.onef[:], [[-1, 128]], ALU.is_equal, 0.0, 0, 1), 128, ["onef"], ["identf"])
    if 16 in sig:
        cp(T.identh[:], T.identf[:], ["identf"], ["identh"], 128)
    send("A0", judge[0], la[0][:], T.tab[:, 0:128], ["tA0"], ["la0"], 0, 3500)
    pool(lambda: g.iota(T.mi[:], [[-1, 256]], 256, 1), 256, [], ["mi"])
    send("A1", judge[1], la[1][:], T.tab[:, 128:256], ["tA1"], ["la1"], 1, 3500)
    ms(T.big[:], 8192.0, ["big"], 128)
    pool(lambda: g.affine_select(T.upp[:], T.big[:], [[-1, 128]], ALU.is_ge, 0.0, 0, 1), 128, ["big"], ["upp"])
    pool(lambda: g.affine_select(T.sg[:], T.ones[:], [[-16, 8], [0, 128]], ALU.is_equal, 0.0, 0, 1), 1024, ["ones", "onesb"], ["sg"])
    pool(lambda: g.iota(T.dump[:], [[0, 2], [1, 128]], H, 0, allow_small_or_imprecise_dtypes=True), 256, [], ["dump"])
    cp(T.wf[:], T.hwi[:, 0:1], ["hwi"], ["wf"], 1)
    act(T.wblk[:], T.b16[:], ACT.Identity, ["b16", "wf"], ["wblk"], 128, scale=T.wf[:, 0:1])
    ts(T.w8[:, 0:8], T.b16[:, 0:128:16], T.wf[:, 0:1], ALU.mult, ["b16", "wf"], ["w8a"], 8)
    act(T.w8[:, 8:16], T.w8[:, 0:8], ACT.Copy, ["w8a"], ["w8b"], 8, scale=1.0 / 256)
    for c in range(nch):
        j = 1 if sig[c] == 8 else 2
        if sig[c] not in sig[:c]:
            ts(T.pi[:, j:j + 1], T.pi[:, 0:1], 4 if sig[c] == 8 else 3, ALU.arith_shift_right, ["pi"], ["pi%d" % j], 1)
        ts(T.mo[:, c:c + 1], T.pi[:, j:j + 1], 2.0, ALU.mult, ["pi%d" % j], ["mo%d" % c], 1, 2.0 * CH[c][0] + 1, ALU.add)
    MO = ["mo%d" % c for c in range(nch)]
    act(T.acol[:, 0:nch], T.mo[:, 0:nch], ACT.Copy, MO, ["acol"], nch, scale=16.0)
    act(T.acol2[:, 0:nch], T.mo[:, 0:nch], ACT.Identity, MO, ["acol2"], nch, scale=16.0, bias=2048.0)
    if XACT:
        act(T.i256n[:], T.identf[:], ACT.Copy, ["identf"], ["i256n"], 128, scale=-256.0)
    act(T.k0[:, 0:nch], T.mo[:, 0:nch], ACT.Square, MO, ["k0"], nch)
    for d in range(S):
        act(T.kcol[:, NC * d:NC * d + nch], T.k0[:, 0:nch], ACT.Identity, ["k0"], ["kcol%d" % d], nch, scale=-8.0, bias=811.0 * d - DELTA)
    act(T.ident[:], T.identf[:], ACT.Copy, ["identf"], ["ident"], 128)
    act(T.i256[:], T.identf[:], ACT.Copy, ["identf"], ["i256"], 128, scale=256.0)
    act(T.ineg[:], T.identf[:], ACT.Copy, ["identf"], ["ineg"], 128, scale=-2.0 ** 21)
    ts(T.mi[:], T.mi[:], 15, ALU.bitwise_and, ["mi"], ["mi"], 256)
    ts(T.m16[:], T.mi[:], 0.0, ALU.is_equal, ["mi"], ["m16"], 256)
    ms(T.rst[:], 1.0, ["rst"], 512)
    ms(T.rst[:, 0:256:16], 0.0, ["rst"], 32)
    ms(T.z2[:], 0.0, ["z2"], 240)
    ms(T.z2[:, 112:128], 1.0, ["z2"], 16)
    act(T.bmf[:], T.b16[:, 0:128:16], ACT.Copy, ["b16"], ["bmf"], 8)
    for j, s in ((0, 1.0), (1, 1.0), (2, -1.0), (3, 0.0), (4, -1.0)):
        act(T.ob[:, 8 * j:8 * j + 8], T.bmf[:], ACT.Copy, ["bmf"], ["ob%d" % j], 8, scale=s)
    for k in range(8):
        act(T.qblk[:, 16 * k:16 * k + 16], T.mixs[:], ACT.Identity, ["mixs", "bmf"], ["qb%d" % k], 16, scale=T.bmf[:, k:k + 1])
    OB, QB = ["ob%d" % j for j in range(5)], ["qb%d" % k for k in range(8)]
    ts(T.negt[:], T.goi[:, 0:1], -1.0, ALU.mult, ["goi"], ["negt"], 1)

    def chain(c, d, src, srck, tmp, col, kt, banks, dst, dstk):
        m0, n = CH[c]
        W, J = 8 * sig[c], 8 * n
        P = 128 * n // sig[c]
        xi, vf = T.xi[0:P, 128 * tmp:128 * tmp + W], T.vf[0:P, 128 * tmp:128 * tmp + W]
        kx, kv, kp = "xi%d" % tmp, "vf%d" % tmp, "pad%d" % tmp
        if src is None:
            act(vf, vf, ACT.Square, [kv, "acol2"], [kv], W, bias=T.acol2[0:P, c:c + 1])
        else:
            ts(vf, src, T.acol[0:P, c:c + 1], ALU.add, [srck, "acol"], [kv], W)
            act(vf, vf, ACT.Square, [kv], [kv], W)
        ts(xi, vf, 1.0 / 32, ALU.mult, [kv, "kcol%d" % d], [kx], W, T.kcol[0:P, NC * d + c:NC * d + c + 1], ALU.add)
        ts(xi, xi, V - 1, ALU.bitwise_and, [kx], [kx], W)
        tr = ps[:, col:col + J]
        if sig[c] == 8:
            b = 17 * tmp
            ts(T.pad[0:P, b + 1:b + 17:2, :], xi, -2048.0, ALU.add, [kx], [kp], W)
            mm([(tr, T.pad[0:P, b + 1:b + 17, :], T.selh[0:P, 0:J], True, False, 64),
                (tr, T.pad[0:P, b:b + 16, :], T.selh[0:P, 64:64 + J], False, True, 64)], [kp, "selh"], [kt], banks)
        else:
            hf = T.hf[:, 128 * tmp:128 * tmp + 128]
            ts(hf, xi, -2048.0, ALU.add, [kx], [kp], W)
            mm([(tr, hf, T.identh[:], True, True, 128)], [kp, "identh"], [kt], banks)
        ts(dst[:, 8 * m0:8 * m0 + J], tr, 2048.0, ALU.add, [kt], [dstk, kt], J, banks=banks)

    def step0(t):
        a, r = la[t], arep[t]
        k = "arep%d" % t
        cp(r[:, 0:128], a[:], ["la%d" % t], [k + "a"], 128, c=0.5)
        cp(r[:, 128:256], a[:], ["la%d" % t], [k + "b"], 128, c=0.5)
        ks, w = [k + "a", k + "b"], 256
        while w < 128 * max(sig):
            cp(r[:, w:2 * w], r[:, 0:w], ks, [k + str(w)], w, c=0.5)
            ks, w = ks + [k + str(w)], 2 * w
        for sg_ in sorted(set(sig), reverse=True):
            kl, col = lease()
            v, kv = (T.v8, "v8") if sg_ == 8 else (T.v16, "v16")
            mm([(ps[:, col + s:col + 8 * sg_:sg_], r[:, s:128 * sg_:sg_], T.w8[:, 0:8], True, True, 64) for s in range(sg_)], ks + ["w8a"], [kl])
            cp(v[:], ps[:, col:col + 8 * sg_], [kl], [kv, kl], 8 * sg_)
            ts(v[:], v[:], V - 1, ALU.bitwise_and, [kv], [kv], 8 * sg_)
        for c in range(nch):
            kl, col = lease()
            v, kv = (T.v8, "v8") if sig[c] == 8 else (T.v16, "v16")
            chain(c, 0, v[0:128 * CH[c][1] // sig[c], :], kv, NC + c, col, kl, [], o0[t], "o0%d%d" % (t, c))
        ts(T.aht[:], a[:], 0.0, ALU.is_equal, ["la%d" % t], ["aht"], 128, 4096.0, ALU.mult, c=0.5)
        tt(ah[t][:], T.aht[:], a[:], ALU.add, ["aht", "la%d" % t], ["ah%d" % t], 128)
        return ks

    RA = [step0(0)]

    kl, col = lease()
    mm([(ps[:, col:col + 256], T.wblk[:], T.tab[:, 0:256], True, True, 256)], ["wblk", "tA0", "tA1"], [kl])
    cp(T.ui[:], ps[:, col:col + 256], [kl], ["ui", kl], 256)
    ts(T.ui[:], T.ui[:], V - 1, ALU.bitwise_and, ["ui"], ["ui"], 256)
    ts(T.uf[:], T.ui[:], 592.0, ALU.add, ["ui"], ["uf"], 256)
    act(T.uf[:], T.uf[:], ACT.Square, ["uf"], ["uf"], 256)
    ts(T.bi[:], T.uf[:], 1.0 / 32, ALU.mult, ["uf"], ["bi"], 256, -8.0 * 37 * 37 - DELTA, ALU.add)
    ts(T.bi[:], T.bi[:], H - 1, ALU.bitwise_and, ["bi"], ["bi"], 256)
    cp(T.bfl[:], T.bi[:], ["bi"], ["bfl"], 256)
    act(T.xy[:, 0:256], T.bfl[:], ACT.Copy, ["bfl"], ["xh"], 256)
    tt(T.xy[:, 256:512], T.bfl[:], T.xy[:, 0:256], ALU.subtract, ["bfl", "xh"], ["xl"], 256)
    act(T.nxy[:], T.xy[:], ACT.Copy, ["xh", "xl"], ["nxy"], 512, scale=-1.0)
    for t in range(RO):
        for hf in range(2):
            e = 2 * t + hf
            kl, col = lease()
            lst = []
            for k in range(4):
                gq = 4 * hf + k
                o = ps[:, col + 128 * k:col + 128 * k + 128]
                s_ = T.sg[:, 128 * gq:128 * gq + 128]
                c0, c1 = 128 * t, 256 + 128 * t
                lst += [(o, s_, T.xy[:, c0:c0 + 128], True, False, 128), (o, s_, T.xy[:, c1:c1 + 128], False, False, 128),
                        (o, T.nxy[:, c0:c0 + 128], s_, False, False, 128), (o, T.nxy[:, c1:c1 + 128], s_, False, False, 128),
                        (o, T.ident[:], T.upp[:], False, True, 128)]
            mm(lst, ["sg", "xh", "xl", "nxy", "ident", "upp"], [kl])
            ts(T.eq[:, 512 * e:512 * e + 512], ps[:, col:col + 512], 0.0, ALU.is_equal, [kl], ["eq%d" % e, kl], 512)
        kl, col = lease()
        o = ps[:, col:col + 128]
        mm([(o, T.z2[:, 112 - 16 * k:240 - 16 * k], T.eq[:, 1024 * t + 128 * k:1024 * t + 128 * k + 128], k == 0, k == 7, 128) for k in range(8)],
           ["z2", "eq%d" % (2 * t), "eq%d" % (2 * t + 1)], [kl])
        ts(T.fst[:, 128 * t:128 * t + 128], o, 0.0, ALU.is_equal, [kl], ["fst%d" % t, kl], 128)
    tt(T.t1[:], T.bfl[:], T.m16[:], ALU.mult, ["bfl", "m16"], ["t1"], 256)
    add("dve", [lambda: ve.tensor_tensor_scan(T.t2[:], T.rst[:], T.t1[:], 0.0, ALU.mult, ALU.add)], vd(256), ["t1", "rst"], ["t2"])
    cp(T.offb[:], T.t2[:, 15:256:16], ["t2"], ["offb"], 16)
    ts(T.upar[:], T.ui[:], 1, ALU.bitwise_and, ["ui"], ["upar"], 256)
    ts(T.thr[:], T.upar[:], 2.0, ALU.mult, ["upar"], ["thr"], 256, 9.0, ALU.add)
    tt(T.t3[:], T.bfl[:], T.dump[:], ALU.subtract, ["bfl", "dump"], ["t3"], 256)
    tt(T.t3[:], T.t3[:], T.fst[:], ALU.mult, ["t3", "fst0", "fst1"], ["t3"], 256)
    tt(T.t3[:], T.t3[:], T.dump[:], ALU.add, ["t3", "dump"], ["t3"], 256)
    tt(T.t3[:], T.t3[:], T.m16[:], ALU.mult, ["t3", "m16"], ["t3"], 256)
    add("dve", [lambda: ve.tensor_tensor_scan(T.t4[:], T.rst[:], T.t3[:], 0.0, ALU.mult, ALU.add)], vd(256), ["t3", "rst"], ["t4"])
    cp(T.offs[:], T.t4[:, 15:256:16], ["t4"], ["offs"], 16)
    ts(T.ma[:], T.tab[:, 0:256], 0.0, ALU.is_equal, ["tA0", "tA1"], ["ma"], 256, c=0.5)

    win = T.tab[:, 0:V]
    nabs = [0]
    for t in range(RO):
        bias[0] = 0.0
        A = T.tab[:, 128 * t:128 * t + 128]
        kA = "tA%d" % t
        p = pk[t]
        k = "pk%d" % t
        act(p[:, 128:256], T.tab[:, H:V].indirect(T.offb[:, 8 * t:8 * t + 8]), ACT.Copy, ["thi", "offb"], [k + "b"], 128, c=GA)
        tt(T.d1[:], p[:, 128:256], T.ma[:, 128 * t:128 * t + 128], ALU.mult, [k + "b", "ma"], ["d1"], 128)
        tt(p[:, 0:128], T.d1[:], A, ALU.add, ["d1", kA], [k + "a"], 128)
        send("B%d" % t, judge[t], lb[t][:], p[:], [k + "a", k + "b"], ["lb%d" % t], None, 3000)
        tt(T.daf[:, 128 * t:128 * t + 128], T.d1[:], T.fst[:, 128 * t:128 * t + 128], ALU.mult, ["d1", "fst%d" % t], ["daf%d" % t], 128)
        kb = "lb%d" % t
        act(T.rep[:, 0, :], arep[t][:, 0:512], ACT.Copy, RA[t], ["repA"], 512)
        for j in range(2):
            act(T.rep[:, j + 1, 0:128], lb[t][:, 128 * j:128 * j + 128], ACT.Copy, [kb], ["repa%d" % j], 128)
            act(T.rep[:, j + 1, 128:256], lb[t][:, 128 * j:128 * j + 128], ACT.Copy, [kb], ["repb%d" % j], 128)
            act(T.rep[:, j + 1, 256:512], T.rep[:, j + 1, 0:256], ACT.Copy, ["repa%d" % j, "repb%d" % j], ["repc%d" % j], 256)
        tile = [T.rep[:, j, :] for j in range(3)]
        tk = [["repA"], ["repa0", "repb0", "repc0"], ["repa1", "repb1", "repc1"]]
        for j in range(3):
            act(T.msk[:, 512 * j:512 * j + 512], tile[j], ACT.Relu, tk[j], ["msk%d" % j], 512, scale=-1.0, bias=1.0)

        def steps(c):
            m0, n = CH[c]
            sg_ = sig[c]
            C, P, J, c0, W = 128 * n, 128 * n // sg_, 8 * n, 128 * m0, 8 * sg_
            us = list(range(m0 // 4, (m0 + n) // 4))
            ko = "off%d" % c
            bank, hn = reg[c]
            hy = hn + W
            for d in range(S):
                n0 = V * d
                bias[0] = BIAS[c] + SB[d]
                step = 512 if d == 0 else min(GS, C)
                for x0 in range(c0, c0 + C, step):
                    uu = list(range(x0 // 512, (x0 + step) // 512))
                    kn = ["n%d%d" % (d, u) for u in uu]
                    nn = T.nb[:, n0 + x0:n0 + x0 + step]
                    if d == 0:
                        src = win.indirect(o0[t][:, x0 // 16:(x0 + step) // 16])
                        if G0ENG[uu[0]] == "dve":
                            cp(nn, src, TAB + ["o0%d%d" % (t, c)], kn, step, c=GA)
                        else:
                            act(nn, src, ACT.Copy, TAB + ["o0%d%d" % (t, c)], kn, step, c=GA)
                    else:
                        tt(nn, win.indirect(T.off[:, x0 // 16:(x0 + step) // 16]), T.yb[:, x0:x0 + step], ALU.min,
                           TAB + [ko] + ["y%d" % u for u in uu], kn, step, c=GA)
                if d == S - 1:
                    if c == 0:
                        act(T.don[:], win.indirect(T.off[:, 0:8]), ACT.Copy, TAB + [ko], ["don"], 128, c=GA)
                        tt(ret[t][:, 0:128], T.don[:], lb[t][:, 128:256], ALU.subtract, ["don", kb], ["ret%da" % t], 128)
                    break
                kn = ["n%d%d" % (d, u) for u in us]
                for u in us:
                    kl, col = lease()
                    o = ps[:, col:col + 512]
                    lst = [(o, T.ineg[:], T.nb[:, n0 + 512 * u:n0 + 512 * u + 512], True, False, 512)]
                    if d == 0:
                        lst += [(ps[:, col + 128 * i:col + 128 * i + 128], T.i256[:], ah[t][:], False, i == 3, 128) for i in range(4)]
                        mm(lst, ["n%d%d" % (d, u), "ineg", "i256", "ah%d" % t], [kl])
                    else:
                        lst += [(o, T.ident[:], T.yb[:, 512 * u:512 * u + 512], False, True, 512)]
                        mm(lst, ["n%d%d" % (d, u), "ineg", "ident", "y%d" % u], [kl])
                    act(T.yb[:, 512 * u:512 * u + 512], o, ACT.Relu, [kl], ["y%d" % u, kl], 512)
                cs = T.cs[0:P, 128 * c:128 * c + W]
                car = CSA and d > 0
                mm([(ps[0:P, hn:hn + W], T.identf[0:P, 0:P], cs, True, False, 4 * W)] * car +
                   [(ps[0:P, hn + s:hn + W:sg_], T.nb[:, n0 + c0 + s:n0 + c0 + C:sg_], T.w8[:, 0:8], not car, s == sg_ - 1 or not car, 64)
                    for s in range(sg_)], kn + ["w8a", "identf"] + ["cs%d" % c] * car, ["hn%d" % c], [bank])
                if d == 0 or CSA:
                    act(cs, ps[0:P, hn:hn + W], ACT.Identity, ["hn%d" % c], ["cs%d" % c], W, banks=[bank],
                        bias=-2048.0 if MOD1 and d == 0 else 0.0)
                else:
                    tt(cs, ps[0:P, hn:hn + W], cs, ALU.add, ["hn%d" % c, "cs%d" % c], ["cs%d" % c], W, banks=[bank], c=1.0)
                mm([(ps[0:P, hy + s:hy + W:sg_], T.yb[:, c0 + s:c0 + C:sg_], T.w8[:, 8:16], True, True, 64) for s in range(sg_)],
                   ["y%d" % u for u in us] + ["w8b"], ["hy%d" % c], [bank])
                xi = T.xi[0:P, 128 * c:128 * c + W]
                if MOD1:
                    x, rr = ps[0:P, hy:hy + W], T.rr[0:P, 128 * c:128 * c + W]
                    tt(x, x, cs, ALU.add, ["hy%d" % c, "cs%d" % c], ["hy%d" % c], W, banks=[bank], c=1.0)
                    act(rr, x, ACT.Identity, ["hy%d" % c], ["rr%d" % c], W, banks=[bank], bias=M12)
                    act(rr, rr, ACT.Identity, ["rr%d" % c], ["rr%d" % c], W, bias=-M12)
                    tt(T.vf[0:P, 128 * c:128 * c + W], x, rr, ALU.subtract, ["hy%d" % c, "rr%d" % c], ["vf%d" % c], W, banks=[bank], c=1.0)
                    chain(c, d + 1, None, None, c, hy, "hy%d" % c, [bank], T.off, ko)
                else:
                    tt(xi, ps[0:P, hy:hy + W], cs, ALU.add, ["hy%d" % c, "cs%d" % c], ["xi%d" % c], W, banks=[bank], c=1.0)
                    ts(xi, xi, V - 1, ALU.bitwise_and, ["xi%d" % c], ["xi%d" % c], W)
                    chain(c, d + 1, xi, "xi%d" % c, c, hy, "hy%d" % c, [bank], T.off, ko)
                if 1 <= d <= NADD:
                    k0 = ["n0%d" % u for u in us]
                    add("pool", [lambda d=d: g.dma_start(T.nb[:, c0:c0 + C], T.nb[:, V * d + c0:V * d + c0 + C], accum_op=ALU.add)],
                        DQ, kn + k0, k0, kind="d", sem="ad%d%d%d" % (t, c, d), cnt=16, lat=2000 + 2.0 * C)
                if t == 0 and c == 0 and d == 1:
                    dma("sp", T.y[:, 256:H], T.tab[:, 256:H], ["tlo"] + kn, [], "ylo", 5000)

        def verdict(u):
            kl, col = lease()
            o = ps[:, col:col + 512]
            ds = [0] + list(range(NADD + 1, S))
            mm([(o, T.ident[:], T.nb[:, V * d + 512 * u:V * d + 512 * u + 512], d == 0, d == S - 1, 512) for d in ds],
               ["n%d%d" % (d, u) for d in ds] + ["ident"], [kl])
            xa = min(3, (XACT + 7 - u) // 8)
            for j in range(xa, 3):
                tt(T.xs[:, j, 512 * u:512 * u + 512], o, T.msk[:, 512 * j:512 * j + 512], ALU.mult,
                   [kl, "msk%d" % j], ["x%d%d" % (j, u), kl], 512, c=1.0)
            for j in range(xa):
                kl, col = lease()
                o = ps[:, col:col + 512]
                mm([(o, T.i256n[:], tile[j], True, False, 512)] +
                   [(o, T.ident[:], T.nb[:, V * d + 512 * u:V * d + 512 * u + 512], False, d == S - 1, 512) for d in ds],
                   ["n%d%d" % (d, u) for d in ds] + ["ident", "i256n"] + tk[j], [kl])
                act(T.xs[:, j, 512 * u:512 * u + 512], o, ACT.Relu, [kl], ["x%d%d" % (j, u), kl], 512)
            if u < XDMA:
                kx = ["x%d%d" % (j, u) for j in range(3)]
                add("pool", [lambda: g.dma_start(T.xs[:, :, 512 * u:512 * u + 512], T.rep[:], accum_op=ALU.add)],
                    1000, kx + tk[0] + tk[1] + tk[2], kx, kind="d", sem="ax%d%d" % (t, u), cnt=16, lat=5000)
            st = nabs[0] % 3
            for j in range(3):
                kl, col = lease()
                o = ps[:, col:col + 512]
                ka = "ab%d%d" % (st, j)
                mm([(o, T.qblk[:], tile[j], True, False, 512)] * (u >= XDMA) + [(o, T.qblk[:], T.xs[:, j, 512 * u:512 * u + 512], u < XDMA, True, 512)],
                   QB + tk[j] + ["x%d%d" % (j, u)], [kl, ka])
                a0 = 512 * (3 * st + j)
                act(T.ab[:, a0:a0 + 512], o, ACT.Abs, [kl, "negt"], [ka, kl], 512, bias=T.negt[:, 0:1])
            r = nabs[0] % 2
            dq = 3968 + 64 * r
            for q in range(4):
                o = ps[:, dq + q:dq + 64:4]
                a0 = 512 * 3 * st + 128 * q
                mm([(o, T.ab[:, a0 + 512:a0 + 640], T.ob[:, 0:16], True, False, 256),
                    (o, T.ab[:, a0:a0 + 128], T.ob[:, 16:32], False, False, 256),
                    (o, T.ab[:, a0 + 1024:a0 + 1152], T.ob[:, 24:40], False, True, 256)],
                   OB + ["ab%d%d" % (st, j) for j in range(3)], ["dq%d%d" % (r, q)], [7])
            w = T.wg[:, 64 * r:64 * r + 64]
            act(w, ps[:, dq:dq + 64], ACT.Sign, ["dq%d%d" % (r, q) for q in range(4)], ["wg%d" % r], 64, banks=[7], bias=-0.5)
            hf, mo = u // 4, 4 * (u % 4)
            tt(T.worse[:, 8 * hf:8 * hf + 8, mo:mo + 4], T.wg[:, 64 * r:64 * r + 32], T.wg[:, 64 * r + 32:64 * r + 64], ALU.max,
               ["wg%d" % r], ["worse%d" % u], 32)
            nabs[0] += 1
            if u % 4 == 3:
                kl, col = lease()
                o = ps[:, col:col + 128]
                mm([(o, T.worse[:, 8 * hf:8 * hf + 8, :], T.ident[:], True, True, 128)], ["worse%d" % (4 * hf + i) for i in range(4)] + ["ident"], [kl])
                act(T.wt[:, 128 * hf:128 * hf + 128], o, ACT.Copy, [kl], ["wt%d" % hf, kl], 128)

        for c in range(nch):
            bias[0] = BIAS[c]
            steps(c)
        bias[0] = 0.0
        if t + 1 < RO:
            RA.append(step0(t + 1))
        for u in range(8):
            bias[0] = VB + UB[u] + [BIAS[c] for c in range(nch) if CH[c][0] <= 4 * u][-1]
            verdict(u)
        bias[0] = 0.0
        kl, col = lease()
        o = ps[:, col:col + 128]
        mm([(o, T.b16[:], T.wt[:, 0:128], True, False, 128), (o, T.b16[:], T.wt[:, 128:256], False, True, 128)], ["b16", "wt0", "wt1"], [kl])
        cp(ret[t][:, 128:256], o, [kl], ["ret%db" % t, kl], 128)
        send("R%d" % t, home[t], lr[t][:], ret[t][:], ["ret%da" % t, "ret%db" % t], ["lr%d" % t], None, 2500)
        kr = "lr%d" % t
        tt(T.fz[:], lr[t][:, 128:256], T.thr[:, 128 * t:128 * t + 128], ALU.is_le, [kr, "thr"], ["fz"], 128)
        tt(T.tb[:], T.fz[:], lr[t][:, 0:128], ALU.mult, [kr, "fz"], ["tb"], 128)
        tt(T.tab[:, H:V + L].indirect(T.offs[:, 8 * t:8 * t + 8]), T.tb[:], p[:, 128:256], ALU.add, ["tb", k + "b", "offs"], ["thi"], 128, c=4.0)
        tt(T.ta[:], T.fz[:], T.daf[:, 128 * t:128 * t + 128], ALU.mult, ["fz", "daf%d" % t], ["ta"], 128)
        tt(A, T.ta[:], A, ALU.add, ["ta", kA], [kA], 128)
        dma("act" if t else "sp", T.y[:, 128 * t:128 * t + 128], A, [kA], [], "yA%d" % t, 2500)
    dma("sp", T.y[:, H:V], T.tab[:, H:V], ["thi"], [], "yhi", 5000)
    return ops


def order(ops):
    n = len(ops)
    lastw, readers, first, last = {}, {}, {}, {}
    deps = [dict() for _ in range(n)]
    for i, o in enumerate(ops):
        for k in o["r"]:
            if k in lastw:
                j, via = lastw[k]
                deps[i][j] = via if deps[i].get(j) != "r" else "r"
        for k in o["w"] + o["land"]:
            if k in lastw:
                deps[i].setdefault(lastw[k][0], lastw[k][1])
            for j in readers.get(k, ()):
                if j != i:
                    deps[i].setdefault(j, "s")
            if k[0] == "L":
                first.setdefault(k, i)
                last[k] = i
        for k in o["r"]:
            readers.setdefault(k, []).append(i)
        for k in o["w"]:
            lastw[k] = (i, "s")
            readers[k] = []
        for k in o["land"]:
            lastw[k] = (i, "r")
            readers[k] = []
    acq = {i: k for k, i in first.items()}
    rel = {i: k for k, i in last.items()}
    succ = [[] for _ in range(n)]
    for i in range(n):
        for j in deps[i]:
            succ[j].append(i)
    pr = [0.0] * n
    for i in range(n - 1, -1, -1):
        pr[i] = ops[i]["dur"] + ops[i]["lat"] + max([pr[j] + HOP for j in succ[i]] + [0.0])
    left = [len(d) for d in deps]
    ready = [i for i in range(n) if left[i] == 0]
    fin, free, blast, seq, assign = [0.0] * n, {}, {}, [], {}
    spare = {b: None for b in range(6)}

    def when(b):
        return 0.0 if spare[b] is None else fin[spare[b]] + HOP

    def start(i):
        o = ops[i]
        s = free.get(o["eng"], 0.0)
        for j in deps[i]:
            if not (o["eng"] == "pe" and ops[j]["eng"] == "pe"):
                s = max(s, fin[j] + HOP)
        for b in o["banks"]:
            for e, j in blast.get(b, {}).items():
                if e != o["eng"]:
                    s = max(s, fin[j] + HOP)
        if i in acq:
            s = max(s, min(when(b) for b in spare))
        return s
    while ready:
        st = [(start(i), i) for i in ready if spare or i not in acq]
        lo = min(st)[0]
        s, i = max([x for x in st if x[0] <= lo + WINDOW], key=lambda x: (pr[x[1]] + ops[x[1]]["bias"], -x[1]))
        o = ops[i]
        for b in o["banks"]:
            for e, j in blast.get(b, {}).items():
                if e != o["eng"]:
                    deps[i].setdefault(j, "s")
            blast.setdefault(b, {})[o["eng"]] = i
        if i in acq:
            b = min(spare, key=when)
            if spare[b] is not None:
                deps[i].setdefault(spare[b], "s")
            del spare[b]
            assign[acq[i]] = b
        free[o["eng"]] = s + o["dur"]
        fin[i] = s + o["dur"] + o["lat"]
        if i in rel:
            spare[assign[rel[i]]] = i
        o["t0"] = s
        seq.append(i)
        ready.remove(i)
        for j in succ[i]:
            left[j] -= 1
            if left[j] == 0:
                ready.append(j)
    return seq, deps, assign, max(fin)


def rank_program(g, core, T, topo):
    if T.rank_of(core) is None:
        return
    seq, deps, assign, _ = order(build(g, core, T, topo, {}))
    ops = build(g, core, T, topo, assign)
    Q = {"pe": g.tensor, "dve": g.vector, "act": g.scalar, "pool": g, "sp": g.sync}
    count, mark, waited = {}, {}, {}
    for i in seq:
        o = ops[i]
        e = o["eng"]
        need = {}
        for j, via in deps[i].items():
            p = ops[j]
            if p["kind"] == "c":
                if e == "pe" and p["eng"] == "pe":
                    continue
                s, v = "c" + p["eng"], mark[j]
            elif p["kind"] == "d":
                s, v = p["sem"], 16
            else:
                s, v = via + p["sem"], p["cnt"]
            need[s] = max(need.get(s, 0), v)
        for s, v in need.items():
            if waited.get((e, s), 0) < v:
                Q[e].wait_ge(T.sem[s], v)
                waited[(e, s)] = v
        for fn in o["fns"]:
            ins = fn()
            if o["kind"] == "c":
                ins.then_inc(T.sem["c" + e], 1)
                count[e] = count.get(e, 0) + 1
            elif o["kind"] == "d":
                ins.then_inc(T.sem[o["sem"]], 16)
        mark[i] = count.get(e, 0)
    for e, v in count.items():
        g.wait_ge(T.sem["c" + e], v)
    for o in ops:
        if o["kind"] == "r":
            g.wait_ge(T.sem["s" + o["sem"]], o["cnt"])
            g.wait_ge(T.sem["r" + o["sem"]], o["cnt"])
    for o in ops:
        if o["kind"] == "d":
            g.wait_ge(T.sem[o["sem"]], 16)
